import numpy as np
import ml_dtypes


def mxq(x, axis, fmt="e4m3"):
    dtype, down = {"e4m3": (ml_dtypes.float8_e4m3fn, 7), "e5m2": (ml_dtypes.float8_e5m2, 14)}[fmt]
    v = np.moveaxis(np.asarray(x, np.float32).astype(ml_dtypes.bfloat16).astype(np.float64), axis, -1)
    blocks = v.reshape(v.shape[:-1] + (-1, 32))
    amax = np.abs(blocks).max(-1, keepdims=True)
    byte = np.maximum(np.where(amax > 0, np.frexp(amax)[1] - 1 + 127, 0) - down, 1)
    scale = np.exp2(byte - 127.0)
    codes = (blocks / scale).astype(np.float32).astype(dtype).astype(np.float64)
    return np.moveaxis((codes * scale).reshape(v.shape), -1, axis)


WIDE = False


def mx_kscale(k):
    if not WIDE:
        return np.ones(k)
    levels = np.array([10, -10, 5, -5, 0])
    if k % 512:
        return np.exp2(np.random.permutation(np.resize(levels, k // 32))).repeat(32)
    a = np.empty((k // 512, 16))
    for p in range(k // 512):
        a[p, :8] = np.random.permutation(np.resize(levels, 8))
        for g in range(8):
            far = levels[np.abs(levels - a[p, g]) >= 10]
            a[p, g + 8] = far[np.random.randint(len(far))]
    return np.exp2(a.ravel()).repeat(32)


def f64(x):
    return np.asarray(x).astype(np.float64)


def striped(idx):
    return np.tile(idx.reshape(-1, 16).T, (8, 1)).astype(np.uint16)


def unstriped(offs):
    return offs[:16].T.reshape(-1).astype(np.int64)


def pack_weight(w):
    k, n = w.shape
    w = f64(np.asarray(w, np.float32).astype(ml_dtypes.bfloat16)).reshape(k // 32, 32, n)
    amax = np.abs(w).max(1)
    byte = np.clip(np.where(amax > 0, np.frexp(amax)[1] - 1 + 127 - 7, 1), 1, 254)
    scaled = (w * np.exp2(127.0 - byte)[:, None, :]).reshape(k, n).astype(np.float32)
    words = np.ascontiguousarray(scaled.reshape(k // 512, 128, 4, n).transpose(0, 1, 3, 2)).astype(ml_dtypes.float8_e4m3fn).view(np.uint8)
    return words, np.ascontiguousarray(byte.astype(np.uint8).reshape(k // 512, 16, n))


def unpack_weight(words, scales):
    g, p, n, _ = words.shape
    vals = np.ascontiguousarray(words).view(ml_dtypes.float8_e4m3fn).astype(np.float64) * np.repeat(np.exp2(scales.astype(np.float64) - 127.0), 8, axis=1)[..., None]
    return vals.transpose(0, 1, 3, 2).reshape(g * 512, n)


K, T, E, C, N = 2048, 1024, 8, 256, 128


def by_expert(wq, xq):
    return np.concatenate([wq[e].T @ xq[:, e * C:(e + 1) * C] for e in range(E)], axis=1)


def setup_inputs():
    n = np.random.standard_normal
    s = mx_kscale(K)[:, None]
    first = np.random.permutation(np.repeat(np.arange(E), T // E))
    second = (first + 1 + np.random.permutation(np.repeat(np.arange(E - 1), -(-T // (E - 1)))[:T])) % E
    while np.bincount(second, minlength=E).max() != T // E:
        load = np.bincount(second, minlength=E); hi, lo = int(load.argmax()), int(load.argmin())
        t = np.flatnonzero((second == hi) & (first != lo))[0]; second[t] = lo
    slot_token = np.empty(E * C, np.int64); pos = np.empty((2, T), np.int64); fill = np.zeros(E, np.int64)
    place = np.stack([np.random.permutation(C) for _ in range(E)])
    for r, deal in enumerate((first, second)):
        for t in np.random.permutation(T):
            e = deal[t]; j = e * C + place[e, fill[e]]; fill[e] += 1; slot_token[j] = t; pos[r, t] = j
    g = np.random.uniform(0.2, 0.8, T)
    packed = [pack_weight(m) for m in n((E, K, N)) / np.sqrt(K) / s[None]]
    return {
        "xT": (n((K, T)) * s).astype(np.float32),
        "w_words": np.stack([m[0] for m in packed]),
        "w_scales": np.stack([m[1] for m in packed]),
        "gate": np.stack([np.tile(g, (N, 1)), np.tile(1.0 - g, (N, 1))]).astype(np.float32),
        "offs": striped(slot_token),
        "pos1": striped(pos[0]),
        "pos2": striped(pos[1]),
    }


def reference(xT, w_words, w_scales, gate, offs, pos1, pos2):
    idx = unstriped(offs)
    xq = mxq(f64(xT)[:, idx], 0, "e4m3")
    w = np.stack([unpack_weight(w_words[e], w_scales[e]) for e in range(E)])
    y = by_expert(w, xq)
    return f64(gate[0]) * y[:, unstriped(pos1)] + f64(gate[1]) * y[:, unstriped(pos2)]

@@ -1,0 +1,123 @@
+from contextlib import ExitStack
+
+import concourse.mybir as mybir
+
+K, T, E, C, N = 2048, 1024, 8, 256, 128
+FLOPS = 2 * K * E * C * N
+
+F32 = mybir.dt.float32
+BF16 = mybir.dt.bfloat16
+I32 = mybir.dt.int32
+U8 = mybir.dt.uint8
+U16 = mybir.dt.uint16
+FP8X4 = mybir.dt.float8_e4m3fn_x4
+MULT = mybir.AluOpType.mult
+ADD = mybir.AluOpType.add
+
+P = 128
+PACK = 4
+PASSES = K // (P * PACK)
+SLOTS = E * C
+CHUNK = 512
+CHUNKS = SLOTS // CHUNK
+EXPERTS_A_CHUNK = CHUNK // C
+HALF = 512
+
+
+def tile_routed_moe_kernel(tc, xT, w_words, w_scales, gate, offs, pos1, pos2, out):
+    nc = tc.nc
+    with ExitStack() as ctx:
+        lists = ctx.enter_context(tc.tile_pool(name="lists", bufs=1))
+        keep = ctx.enter_context(tc.tile_pool(name="keep", bufs=1))
+        ring = ctx.enter_context(tc.tile_pool(name="ring", bufs=3))
+        psum = ctx.enter_context(tc.psum_pool(name="psum", bufs=1))
+
+        offs_t = lists.tile([P, SLOTS // 16], U16, name="offs_t")
+        pos1_t = lists.tile([P, T // 16], U16, name="pos1_t")
+        pos2_t = lists.tile([P, T // 16], U16, name="pos2_t")
+        nc.sync.dma_start(offs_t[:], offs)
+
+        x_view = xT.rearrange("(g p t) n -> g p t n", p=P, t=PACK)
+        planes = [[keep.tile([P, T], F32, name="x%d_%d" % (g, t)) for t in range(PACK)] for g in range(PASSES)]
+        w_codes = keep.tile([P, PASSES, E, N], I32, name="w_codes", align_bytes=64)
+        w_planes = keep.tile([P, E * N], U8, name="w_planes", align_bytes=64)
+        w_view = w_words.rearrange("e a p n r -> a p e (n r)")
+        s_view = w_scales.rearrange("e a (q r) n -> a r q e n", r=4)
+
+        nc.vector.memset(w_planes[:].bitcast(I32), 0)
+        for g in range(PASSES):
+            for t in range(PACK):
+                nc.sync.dma_start(planes[g][t][:], x_view[g, :, t, :])
+            if g == 0:
+                for a in range(PASSES):
+                    for r in range(4):
+                        nc.sync.dma_start(
+                            w_planes[4 * a + r : P : 32, :].rearrange("q (e n) -> q e n", e=E).bitcast(I32),
+                            s_view[a, r].bitcast(I32),
+                        )
+            nc.sync.dma_start(w_codes[:, g, :, :], w_view[g].bitcast(I32))
+        nc.sync.dma_start(pos1_t[:], pos1)
+        nc.sync.dma_start(pos2_t[:], pos2)
+        gate_t = keep.tile([P, 2, T], F32, name="gate_t")
+        nc.sync.dma_start(gate_t[:], gate.rearrange("r n t -> n r t"))
+
+        acc = [psum.tile([P, C], F32, name="acc%d" % e) for e in range(E)]
+        y = keep.tile([P, SLOTS], F32, name="y")
+
+        steps = [(g, c) for g in range(PASSES) for c in range(CHUNKS)]
+        gathered = {}
+        grouped = {}
+
+        def gather(i):
+            g, c = steps[i]
+            g4 = ring.tile([P, PACK, CHUNK], F32, name="g4")
+            for t in range(PACK):
+                nc.vector.tensor_copy(
+                    g4[:, t, :], planes[g][t][:].indirect(offs_t[:, c * (CHUNK // 16) : (c + 1) * (CHUNK // 16)])
+                )
+            gathered[i] = g4
+
+        def interleave(i):
+            gr = ring.tile([P, CHUNK, PACK], BF16, name="gr", align_bytes=64)
+            nc.scalar.copy(gr[:], gathered[i][:].rearrange("p t n -> p n t"))
+            grouped[i] = gr
+
+        def multiply(i):
+            g, c = steps[i]
+            codes = ring.tile([P, CHUNK], I32, name="codes", align_bytes=64)
+            scales = ring.tile([P, CHUNK], U8, name="scales", align_bytes=64)
+            nc.vector.quantize_mx(
+                out=codes[:].bitcast(FP8X4), scales=scales[:], in_=grouped[i][:].rearrange("p n t -> p (n t)")
+            )
+            for j in range(EXPERTS_A_CHUNK):
+                e = c * EXPERTS_A_CHUNK + j
+                nc.tensor.matmul_mx(
+                    out=acc[e][:],
+                    lhsT=w_codes[:, g, e, :].bitcast(FP8X4),
+                    lhsT_scale=w_planes[4 * g : P, e * N : (e + 1) * N],
+                    rhs=codes[:, j * C : (j + 1) * C].bitcast(FP8X4),
+                    rhs_scale=scales[:, j * C : (j + 1) * C],
+                    start=(g == 0),
+                    stop=(g == PASSES - 1),
+                )
+                if g == PASSES - 1:
+                    nc.scalar.copy(y[:, e * C : (e + 1) * C], acc[e][:])
+
+        gather(0)
+        interleave(0)
+        for i in range(1, len(steps)):
+            gather(i)
+            interleave(i)
+            multiply(i - 1)
+        multiply(len(steps) - 1)
+
+        for h in range(T // HALF):
+            cols = slice(h * HALF, (h + 1) * HALF)
+            lcols = slice(h * (HALF // 16), (h + 1) * (HALF // 16))
+            z1 = ring.tile([P, HALF], F32, name="z1")
+            z2 = ring.tile([P, HALF], F32, name="z2")
+            nc.vector.tensor_tensor(z1[:], y[:].indirect(pos1_t[:, lcols]), gate_t[:, 0, cols], MULT)
+            nc.vector.tensor_tensor(z2[:], y[:].indirect(pos2_t[:, lcols]), gate_t[:, 1, cols], MULT)
+            res = ring.tile([P, HALF], F32, name="res")
+            nc.vector.tensor_tensor(res[:], z1[:], z2[:], ADD)
+            nc.sync.dma_start(out[:, cols], res[:])

@@ -13,6 +13,7 @@ U16 = mybir.dt.uint16
 FP8X4 = mybir.dt.float8_e4m3fn_x4
 MULT = mybir.AluOpType.mult
 ADD = mybir.AluOpType.add
+COPY = mybir.ActivationFunctionType.Copy
 
 P = 128
 PACK = 4
@@ -22,6 +23,11 @@ CHUNK = 512
 CHUNKS = SLOTS // CHUNK
 EXPERTS_A_CHUNK = CHUNK // C
 HALF = 512
+LIST_COLS = C // 16
+
+PASS_ORDER = (0, 1, 3, 2)
+SCALAR_PASSES = (3, 2)
+SHARED_VECTOR_CHUNKS = 1
 
 
 def tile_routed_moe_kernel(tc, xT, w_words, w_scales, gate, offs, pos1, pos2, out):
@@ -29,7 +35,10 @@ def tile_routed_moe_kernel(tc, xT, w_words, w_scales, gate, offs, pos1, pos2, ou
     with ExitStack() as ctx:
         lists = ctx.enter_context(tc.tile_pool(name="lists", bufs=1))
         keep = ctx.enter_context(tc.tile_pool(name="keep", bufs=1))
-        ring = ctx.enter_context(tc.tile_pool(name="ring", bufs=3))
+        vring = ctx.enter_context(tc.tile_pool(name="vring", bufs=4))
+        sring = ctx.enter_context(tc.tile_pool(name="sring", bufs=7))
+        qring = ctx.enter_context(tc.tile_pool(name="qring", bufs=8))
+        tail = ctx.enter_context(tc.tile_pool(name="tail", bufs=2))
         psum = ctx.enter_context(tc.psum_pool(name="psum", bufs=1))
 
         offs_t = lists.tile([P, SLOTS // 16], U16, name="offs_t")
@@ -38,23 +47,27 @@ def tile_routed_moe_kernel(tc, xT, w_words, w_scales, gate, offs, pos1, pos2, ou
         nc.sync.dma_start(offs_t[:], offs)
 
         x_view = xT.rearrange("(g p t) n -> g p t n", p=P, t=PACK)
-        planes = [[keep.tile([P, T], F32, name="x%d_%d" % (g, t)) for t in range(PACK)] for g in range(PASSES)]
+        raw = [keep.tile([P, PACK, T], F32, name="raw%d" % g) for g in range(PASSES)]
+        xb = dict((g, keep.tile([P, PACK, T], BF16, name="xb%d" % g)) for g in SCALAR_PASSES)
         w_codes = keep.tile([P, PASSES, E, N], I32, name="w_codes", align_bytes=64)
         w_planes = keep.tile([P, E * N], U8, name="w_planes", align_bytes=64)
         w_view = w_words.rearrange("e a p n r -> a p e (n r)")
         s_view = w_scales.rearrange("e a (q r) n -> a r q e n", r=4)
 
         nc.vector.memset(w_planes[:].bitcast(I32), 0)
-        for g in range(PASSES):
+        for t in range(PACK):
+            nc.sync.dma_start(raw[0][:, t, :], x_view[0, :, t, :])
+            nc.sync.dma_start(raw[3][:, t, :], x_view[3, :, t, :])
+        for g in (1, 2):
             for t in range(PACK):
-                nc.sync.dma_start(planes[g][t][:], x_view[g, :, t, :])
-            if g == 0:
-                for a in range(PASSES):
-                    for r in range(4):
-                        nc.sync.dma_start(
-                            w_planes[4 * a + r : P : 32, :].rearrange("q (e n) -> q e n", e=E).bitcast(I32),
-                            s_view[a, r].bitcast(I32),
-                        )
+                nc.sync.dma_start(raw[g][:, t, :], x_view[g, :, t, :])
+        for a in range(PASSES):
+            for r in range(4):
+                nc.sync.dma_start(
+                    w_planes[4 * a + r : P : 32, :].rearrange("q (e n) -> q e n", e=E).bitcast(I32),
+                    s_view[a, r].bitcast(I32),
+                )
+        for g in PASS_ORDER:
             nc.sync.dma_start(w_codes[:, g, :, :], w_view[g].bitcast(I32))
         nc.sync.dma_start(pos1_t[:], pos1)
         nc.sync.dma_start(pos2_t[:], pos2)
@@ -64,31 +77,27 @@ def tile_routed_moe_kernel(tc, xT, w_words, w_scales, gate, offs, pos1, pos2, ou
         acc = [psum.tile([P, C], F32, name="acc%d" % e) for e in range(E)]
         y = keep.tile([P, SLOTS], F32, name="y")
 
-        steps = [(g, c) for g in range(PASSES) for c in range(CHUNKS)]
-        gathered = {}
-        grouped = {}
-
-        def gather(i):
-            g, c = steps[i]
-            g4 = ring.tile([P, PACK, CHUNK], F32, name="g4")
-            for t in range(PACK):
+        def vector_gather(gr, g, c, t):
+            for j in range(EXPERTS_A_CHUNK):
+                e = c * EXPERTS_A_CHUNK + j
                 nc.vector.tensor_copy(
-                    g4[:, t, :], planes[g][t][:].indirect(offs_t[:, c * (CHUNK // 16) : (c + 1) * (CHUNK // 16)])
+                    gr[:, j * C : (j + 1) * C, t],
+                    raw[g][:, t, :].indirect(offs_t[:, e * LIST_COLS : (e + 1) * LIST_COLS]),
                 )
-            gathered[i] = g4
 
-        def interleave(i):
-            gr = ring.tile([P, CHUNK, PACK], BF16, name="gr", align_bytes=64)
-            nc.scalar.copy(gr[:], gathered[i][:].rearrange("p t n -> p n t"))
-            grouped[i] = gr
+        def scalar_gather(gr, g, c, t):
+            for j in range(EXPERTS_A_CHUNK):
+                e = c * EXPERTS_A_CHUNK + j
+                nc.scalar.activation(
+                    gr[:, j * C : (j + 1) * C, t],
+                    xb[g][:, t, :].indirect(offs_t[:, e * LIST_COLS : (e + 1) * LIST_COLS]),
+                    COPY,
+                )
 
-        def multiply(i):
-            g, c = steps[i]
-            codes = ring.tile([P, CHUNK], I32, name="codes", align_bytes=64)
-            scales = ring.tile([P, CHUNK], U8, name="scales", align_bytes=64)
-            nc.vector.quantize_mx(
-                out=codes[:].bitcast(FP8X4), scales=scales[:], in_=grouped[i][:].rearrange("p n t -> p (n t)")
-            )
+        def multiply(gr, g, c):
+            codes = qring.tile([P, CHUNK], I32, name="codes", align_bytes=64)
+            scales = qring.tile([P, CHUNK], U8, name="scales", align_bytes=64)
+            nc.vector.quantize_mx(out=codes[:].bitcast(FP8X4), scales=scales[:], in_=gr[:].rearrange("p n t -> p (n t)"))
             for j in range(EXPERTS_A_CHUNK):
                 e = c * EXPERTS_A_CHUNK + j
                 nc.tensor.matmul_mx(
@@ -97,27 +106,60 @@ def tile_routed_moe_kernel(tc, xT, w_words, w_scales, gate, offs, pos1, pos2, ou
                     lhsT_scale=w_planes[4 * g : P, e * N : (e + 1) * N],
                     rhs=codes[:, j * C : (j + 1) * C].bitcast(FP8X4),
                     rhs_scale=scales[:, j * C : (j + 1) * C],
-                    start=(g == 0),
-                    stop=(g == PASSES - 1),
+                    start=(g == PASS_ORDER[0]),
+                    stop=(g == PASS_ORDER[-1]),
                 )
-                if g == PASSES - 1:
-                    nc.scalar.copy(y[:, e * C : (e + 1) * C], acc[e][:])
 
-        gather(0)
-        interleave(0)
-        for i in range(1, len(steps)):
-            gather(i)
-            interleave(i)
-            multiply(i - 1)
-        multiply(len(steps) - 1)
+        def vector_tiles():
+            return [vring.tile([P, CHUNK, PACK], BF16, name="grv", align_bytes=64) for c in range(CHUNKS)]
+
+        g0 = vector_tiles()
+        for t in range(PACK):
+            for c in range(CHUNKS):
+                vector_gather(g0[c], 0, c, t)
+        g3 = [sring.tile([P, CHUNK, PACK], BF16, name="grs", align_bytes=64) for c in range(CHUNKS)]
+        for t in range(PACK):
+            nc.scalar.copy(xb[3][:, t, :], raw[3][:, t, :])
+            for c in range(CHUNKS):
+                scalar_gather(g3[c], 3, c, t)
+        for c in range(CHUNKS):
+            multiply(g0[c], 0, c)
+        g1 = vector_tiles()
+        for t in range(PACK):
+            for c in range(CHUNKS):
+                vector_gather(g1[c], 1, c, t)
+        for c in range(CHUNKS):
+            multiply(g1[c], 1, c)
+        for t in range(PACK):
+            nc.scalar.copy(xb[2][:, t, :], raw[2][:, t, :])
+        g2 = {}
+        for c in range(SHARED_VECTOR_CHUNKS, CHUNKS):
+            g2[c] = sring.tile([P, CHUNK, PACK], BF16, name="grs", align_bytes=64)
+            for t in range(PACK):
+                scalar_gather(g2[c], 2, c, t)
+        for c in range(CHUNKS):
+            multiply(g3[c], 3, c)
+        for c in range(SHARED_VECTOR_CHUNKS):
+            g2[c] = vring.tile([P, CHUNK, PACK], BF16, name="grv", align_bytes=64)
+            for t in range(PACK):
+                vector_gather(g2[c], 2, c, t)
+        for c in range(CHUNKS - 1):
+            multiply(g2[c], 2, c)
+        for e in range(0, 4):
+            nc.vector.tensor_copy(y[:, e * C : (e + 1) * C], acc[e][:])
+        for e in range(4, 6):
+            nc.scalar.copy(y[:, e * C : (e + 1) * C], acc[e][:])
+        multiply(g2[CHUNKS - 1], 2, CHUNKS - 1)
+        nc.scalar.copy(y[:, 6 * C : 7 * C], acc[6][:])
+        nc.vector.tensor_copy(y[:, 7 * C : 8 * C], acc[7][:])
 
         for h in range(T // HALF):
             cols = slice(h * HALF, (h + 1) * HALF)
             lcols = slice(h * (HALF // 16), (h + 1) * (HALF // 16))
-            z1 = ring.tile([P, HALF], F32, name="z1")
-            z2 = ring.tile([P, HALF], F32, name="z2")
+            z1 = tail.tile([P, HALF], F32, name="z1")
+            z2 = tail.tile([P, HALF], F32, name="z2")
             nc.vector.tensor_tensor(z1[:], y[:].indirect(pos1_t[:, lcols]), gate_t[:, 0, cols], MULT)
             nc.vector.tensor_tensor(z2[:], y[:].indirect(pos2_t[:, lcols]), gate_t[:, 1, cols], MULT)
-            res = ring.tile([P, HALF], F32, name="res")
+            res = tail.tile([P, HALF], F32, name="res")
             nc.vector.tensor_tensor(res[:], z1[:], z2[:], ADD)
             nc.sync.dma_start(out[:, cols], res[:])

@@ -19,15 +19,9 @@ P = 128
 PACK = 4
 PASSES = K // (P * PACK)
 SLOTS = E * C
-CHUNK = 512
-CHUNKS = SLOTS // CHUNK
-EXPERTS_A_CHUNK = CHUNK // C
 HALF = 512
 LIST_COLS = C // 16
-
-PASS_ORDER = (0, 1, 3, 2)
-SCALAR_PASSES = (3, 2)
-SHARED_VECTOR_CHUNKS = 1
+FIRST_PASS, LAST_PASS = 0, 2
 
 
 def tile_routed_moe_kernel(tc, xT, w_words, w_scales, gate, offs, pos1, pos2, out):
@@ -35,8 +29,10 @@ def tile_routed_moe_kernel(tc, xT, w_words, w_scales, gate, offs, pos1, pos2, ou
     with ExitStack() as ctx:
         lists = ctx.enter_context(tc.tile_pool(name="lists", bufs=1))
         keep = ctx.enter_context(tc.tile_pool(name="keep", bufs=1))
+        stage = ctx.enter_context(tc.tile_pool(name="stage", bufs=5))
         vring = ctx.enter_context(tc.tile_pool(name="vring", bufs=4))
-        sring = ctx.enter_context(tc.tile_pool(name="sring", bufs=7))
+        suring = ctx.enter_context(tc.tile_pool(name="suring", bufs=5))
+        sgring = ctx.enter_context(tc.tile_pool(name="sgring", bufs=7))
         qring = ctx.enter_context(tc.tile_pool(name="qring", bufs=8))
         tail = ctx.enter_context(tc.tile_pool(name="tail", bufs=2))
         psum = ctx.enter_context(tc.psum_pool(name="psum", bufs=1))
@@ -47,111 +43,173 @@ def tile_routed_moe_kernel(tc, xT, w_words, w_scales, gate, offs, pos1, pos2, ou
         nc.sync.dma_start(offs_t[:], offs)
 
         x_view = xT.rearrange("(g p t) n -> g p t n", p=P, t=PACK)
-        raw = [keep.tile([P, PACK, T], F32, name="raw%d" % g) for g in range(PASSES)]
-        xb = dict((g, keep.tile([P, PACK, T], BF16, name="xb%d" % g)) for g in SCALAR_PASSES)
+        raw = dict((g, keep.tile([P, PACK, T], F32, name="raw%d" % g)) for g in (0, 1))
+        xb = dict((g, keep.tile([P, PACK, T], BF16, name="xb%d" % g)) for g in (3, 2))
+        staged = {}
         w_codes = keep.tile([P, PASSES, E, N], I32, name="w_codes", align_bytes=64)
         w_planes = keep.tile([P, E * N], U8, name="w_planes", align_bytes=64)
         w_view = w_words.rearrange("e a p n r -> a p e (n r)")
         s_view = w_scales.rearrange("e a (q r) n -> a r q e n", r=4)
-
-        nc.vector.memset(w_planes[:].bitcast(I32), 0)
-        for t in range(PACK):
-            nc.sync.dma_start(raw[0][:, t, :], x_view[0, :, t, :])
-            nc.sync.dma_start(raw[3][:, t, :], x_view[3, :, t, :])
-        for g in (1, 2):
-            for t in range(PACK):
-                nc.sync.dma_start(raw[g][:, t, :], x_view[g, :, t, :])
-        for a in range(PASSES):
-            for r in range(4):
-                nc.sync.dma_start(
-                    w_planes[4 * a + r : P : 32, :].rearrange("q (e n) -> q e n", e=E).bitcast(I32),
-                    s_view[a, r].bitcast(I32),
-                )
-        for g in PASS_ORDER:
-            nc.sync.dma_start(w_codes[:, g, :, :], w_view[g].bitcast(I32))
-        nc.sync.dma_start(pos1_t[:], pos1)
-        nc.sync.dma_start(pos2_t[:], pos2)
         gate_t = keep.tile([P, 2, T], F32, name="gate_t")
-        nc.sync.dma_start(gate_t[:], gate.rearrange("r n t -> n r t"))
-
         acc = [psum.tile([P, C], F32, name="acc%d" % e) for e in range(E)]
         y = keep.tile([P, SLOTS], F32, name="y")
 
-        def vector_gather(gr, g, c, t):
-            for j in range(EXPERTS_A_CHUNK):
-                e = c * EXPERTS_A_CHUNK + j
-                nc.vector.tensor_copy(
-                    gr[:, j * C : (j + 1) * C, t],
-                    raw[g][:, t, :].indirect(offs_t[:, e * LIST_COLS : (e + 1) * LIST_COLS]),
-                )
+        def load_staged(g, t):
+            st = stage.tile([P, T], F32, name="st")
+            nc.sync.dma_start(st[:], x_view[g, :, t, :])
+            staged[(g, t)] = st
 
-        def scalar_gather(gr, g, c, t):
-            for j in range(EXPERTS_A_CHUNK):
-                e = c * EXPERTS_A_CHUNK + j
-                nc.scalar.activation(
-                    gr[:, j * C : (j + 1) * C, t],
-                    xb[g][:, t, :].indirect(offs_t[:, e * LIST_COLS : (e + 1) * LIST_COLS]),
-                    COPY,
-                )
+        def cast(g, t):
+            nc.scalar.copy(xb[g][:, t, :], staged[(g, t)][:])
 
-        def multiply(gr, g, c):
-            codes = qring.tile([P, CHUNK], I32, name="codes", align_bytes=64)
-            scales = qring.tile([P, CHUNK], U8, name="scales", align_bytes=64)
-            nc.vector.quantize_mx(out=codes[:].bitcast(FP8X4), scales=scales[:], in_=gr[:].rearrange("p n t -> p (n t)"))
-            for j in range(EXPERTS_A_CHUNK):
-                e = c * EXPERTS_A_CHUNK + j
+        def start(pool, tag, g, experts):
+            u = pool.tile([P, PACK * C * len(experts)], BF16, name=tag)
+            return (g, experts, u)
+
+        def gather(on_vector, piece, planes):
+            g, experts, u = piece
+            view = u[:].rearrange("p (h n e) -> p h n e", h=2, e=2)
+            for t in planes:
+                for j, e in enumerate(experts):
+                    dst = view[:, t // 2, j * C : (j + 1) * C, t % 2]
+                    lst = offs_t[:, e * LIST_COLS : (e + 1) * LIST_COLS]
+                    if on_vector:
+                        nc.vector.tensor_copy(dst, raw[g][:, t, :].indirect(lst))
+                    else:
+                        nc.scalar.activation(dst, xb[g][:, t, :].indirect(lst), COPY)
+
+        def weave(on_vector, pool, tag, piece):
+            g, experts, u = piece
+            gr = pool.tile([P, PACK * C * len(experts)], BF16, name=tag, align_bytes=64)
+            dst = gr[:].bitcast(F32).rearrange("p (n h) -> p n h", h=2)
+            src = u[:].bitcast(F32).rearrange("p (h n) -> p n h", h=2)
+            if on_vector:
+                nc.vector.tensor_copy(dst, src)
+            else:
+                nc.scalar.copy(dst, src)
+            return (g, experts, gr)
+
+        def multiply(woven):
+            g, experts, gr = woven
+            n = C * len(experts)
+            codes = qring.tile([P, n], I32, name="codes", align_bytes=64)
+            scales = qring.tile([P, n], U8, name="scales", align_bytes=64)
+            nc.vector.quantize_mx(out=codes[:].bitcast(FP8X4), scales=scales[:], in_=gr[:])
+            for j, e in enumerate(experts):
                 nc.tensor.matmul_mx(
                     out=acc[e][:],
                     lhsT=w_codes[:, g, e, :].bitcast(FP8X4),
                     lhsT_scale=w_planes[4 * g : P, e * N : (e + 1) * N],
                     rhs=codes[:, j * C : (j + 1) * C].bitcast(FP8X4),
                     rhs_scale=scales[:, j * C : (j + 1) * C],
-                    start=(g == PASS_ORDER[0]),
-                    stop=(g == PASS_ORDER[-1]),
+                    start=(g == FIRST_PASS),
+                    stop=(g == LAST_PASS),
                 )
 
-        def vector_tiles():
-            return [vring.tile([P, CHUNK, PACK], BF16, name="grv", align_bytes=64) for c in range(CHUNKS)]
+        def take_out(on_vector, e):
+            if on_vector:
+                nc.vector.tensor_copy(y[:, e * C : (e + 1) * C], acc[e][:])
+            else:
+                nc.scalar.copy(y[:, e * C : (e + 1) * C], acc[e][:])
 
-        g0 = vector_tiles()
+        def vector_group(g, pairs):
+            return [start(vring, "uv", g, experts) for experts in pairs]
+
+        def group_gather(group, planes):
+            for t in planes:
+                for piece in group:
+                    gather(True, piece, (t,))
+
+        def group_weave(group):
+            return [weave(True, vring, "grv", piece) for piece in group]
+
+        nc.vector.memset(w_planes[:].bitcast(I32), 0)
         for t in range(PACK):
-            for c in range(CHUNKS):
-                vector_gather(g0[c], 0, c, t)
-        g3 = [sring.tile([P, CHUNK, PACK], BF16, name="grs", align_bytes=64) for c in range(CHUNKS)]
+            nc.sync.dma_start(raw[0][:, t, :], x_view[0, :, t, :])
+            load_staged(3, t)
         for t in range(PACK):
-            nc.scalar.copy(xb[3][:, t, :], raw[3][:, t, :])
-            for c in range(CHUNKS):
-                scalar_gather(g3[c], 3, c, t)
-        for c in range(CHUNKS):
-            multiply(g0[c], 0, c)
-        g1 = vector_tiles()
+            nc.sync.dma_start(raw[1][:, t, :], x_view[1, :, t, :])
+
+        low, high = ((0, 1), (2, 3)), ((4, 5), (6, 7))
+        ga = vector_group(0, low)
+        group_gather(ga, range(PACK))
+
+        s3 = [start(suring, "us", 3, experts) for experts in low + high]
         for t in range(PACK):
-            for c in range(CHUNKS):
-                vector_gather(g1[c], 1, c, t)
-        for c in range(CHUNKS):
-            multiply(g1[c], 1, c)
+            cast(3, t)
+            for piece in s3:
+                gather(False, piece, (t,))
+
         for t in range(PACK):
-            nc.scalar.copy(xb[2][:, t, :], raw[2][:, t, :])
-        g2 = {}
-        for c in range(SHARED_VECTOR_CHUNKS, CHUNKS):
-            g2[c] = sring.tile([P, CHUNK, PACK], BF16, name="grs", align_bytes=64)
-            for t in range(PACK):
-                scalar_gather(g2[c], 2, c, t)
-        for c in range(CHUNKS):
-            multiply(g3[c], 3, c)
-        for c in range(SHARED_VECTOR_CHUNKS):
-            g2[c] = vring.tile([P, CHUNK, PACK], BF16, name="grv", align_bytes=64)
-            for t in range(PACK):
-                vector_gather(g2[c], 2, c, t)
-        for c in range(CHUNKS - 1):
-            multiply(g2[c], 2, c)
+            load_staged(2, t)
+        for a in range(PASSES):
+            for r in range(4):
+                nc.sync.dma_start(
+                    w_planes[4 * a + r : P : 32, :].rearrange("q (e n) -> q e n", e=E).bitcast(I32),
+                    s_view[a, r].bitcast(I32),
+                )
+        for g in (0, 1, 3, 2):
+            nc.sync.dma_start(w_codes[:, g, :, :], w_view[g].bitcast(I32))
+        nc.sync.dma_start(pos1_t[:], pos1)
+        nc.sync.dma_start(pos2_t[:], pos2)
+        nc.sync.dma_start(gate_t[:], gate.rearrange("r n t -> n r t"))
+
+        previous = ga
+        for g, pairs in ((0, high), (1, low), (1, high)):
+            group = vector_group(g, pairs)
+            group_gather(group, (0, 1))
+            woven = group_weave(previous)
+            group_gather(group, (2, 3))
+            for w in woven:
+                multiply(w)
+            previous = group
+            if (g, pairs) == (1, low):
+                w3 = []
+                for t in range(PACK):
+                    w3.append(weave(False, sgring, "grs", s3[t]))
+                    cast(2, t)
+
+        p0 = start(suring, "us", 2, (0, 1))
+        gather(False, p0, range(PACK))
+        p1 = start(suring, "us", 2, (2, 3))
+        gather(False, p1, (0, 1))
+        wp0 = weave(False, sgring, "grs", p0)
+        gather(False, p1, (2, 3))
+
+        wd0 = weave(True, vring, "grv", previous[0])
+        multiply(w3[0])
+        wd1 = weave(True, vring, "grv", previous[1])
+        multiply(w3[1])
+        multiply(wd0)
+        multiply(w3[2])
+        multiply(wd1)
+        multiply(w3[3])
+
+        p2 = start(suring, "us", 2, (4, 5))
+        gather(False, p2, (0, 1))
+        wp1 = weave(False, sgring, "grs", p1)
+        gather(False, p2, (2, 3))
+        p3a = start(suring, "us", 2, (6,))
+        gather(False, p3a, (0, 1))
+        wp2 = weave(False, sgring, "grs", p2)
+        gather(False, p3a, (2, 3))
+        p3b = start(suring, "us", 2, (7,))
+        gather(False, p3b, (0, 1))
+        wp3a = weave(False, sgring, "grs", p3a)
+        gather(False, p3b, (2, 3))
+        wp3b = weave(False, sgring, "grs", p3b)
+
+        multiply(wp0)
+        multiply(wp1)
+        multiply(wp2)
         for e in range(0, 4):
-            nc.vector.tensor_copy(y[:, e * C : (e + 1) * C], acc[e][:])
+            take_out(True, e)
         for e in range(4, 6):
-            nc.scalar.copy(y[:, e * C : (e + 1) * C], acc[e][:])
-        multiply(g2[CHUNKS - 1], 2, CHUNKS - 1)
-        nc.scalar.copy(y[:, 6 * C : 7 * C], acc[6][:])
-        nc.vector.tensor_copy(y[:, 7 * C : 8 * C], acc[7][:])
+            take_out(False, e)
+        multiply(wp3a)
+        take_out(False, 6)
+        multiply(wp3b)
+        take_out(True, 7)
 
         for h in range(T // HALF):
             cols = slice(h * HALF, (h + 1) * HALF)

@@ -31,7 +31,7 @@ def tile_routed_moe_kernel(tc, xT, w_words, w_scales, gate, offs, pos1, pos2, ou
         keep = ctx.enter_context(tc.tile_pool(name="keep", bufs=1))
         stage = ctx.enter_context(tc.tile_pool(name="stage", bufs=5))
         vring = ctx.enter_context(tc.tile_pool(name="vring", bufs=4))
-        suring = ctx.enter_context(tc.tile_pool(name="suring", bufs=5))
+        suring = ctx.enter_context(tc.tile_pool(name="suring", bufs=6))
         sgring = ctx.enter_context(tc.tile_pool(name="sgring", bufs=7))
         qring = ctx.enter_context(tc.tile_pool(name="qring", bufs=8))
         tail = ctx.enter_context(tc.tile_pool(name="tail", bufs=2))
@@ -148,26 +148,30 @@ def tile_routed_moe_kernel(tc, xT, w_words, w_scales, gate, offs, pos1, pos2, ou
                     w_planes[4 * a + r : P : 32, :].rearrange("q (e n) -> q e n", e=E).bitcast(I32),
                     s_view[a, r].bitcast(I32),
                 )
-        for g in (0, 1, 3, 2):
+        for g in (0, 3, 1, 2):
             nc.sync.dma_start(w_codes[:, g, :, :], w_view[g].bitcast(I32))
         nc.sync.dma_start(pos1_t[:], pos1)
         nc.sync.dma_start(pos2_t[:], pos2)
         nc.sync.dma_start(gate_t[:], gate.rearrange("r n t -> n r t"))
 
-        previous = ga
-        for g, pairs in ((0, high), (1, low), (1, high)):
-            group = vector_group(g, pairs)
-            group_gather(group, (0, 1))
-            woven = group_weave(previous)
-            group_gather(group, (2, 3))
-            for w in woven:
-                multiply(w)
-            previous = group
-            if (g, pairs) == (1, low):
-                w3 = []
-                for t in range(PACK):
-                    w3.append(weave(False, sgring, "grs", s3[t]))
-                    cast(2, t)
+        gb = vector_group(0, high)
+        group_gather(gb, (0, 1))
+        wa = group_weave(ga)
+        group_gather(gb, (2, 3))
+        multiply(wa[0])
+        multiply(wa[1])
+
+        for t in range(PACK):
+            cast(2, t)
+
+        gc = vector_group(1, low)
+        group_gather(gc, (0, 1))
+        wb = group_weave(gb)
+        group_gather(gc, (2, 3))
+        multiply(wb[0])
+        multiply(wb[1])
+        w30 = weave(True, sgring, "grs", s3[0])
+        w31 = weave(True, sgring, "grs", s3[1])
 
         p0 = start(suring, "us", 2, (0, 1))
         gather(False, p0, range(PACK))
@@ -176,14 +180,19 @@ def tile_routed_moe_kernel(tc, xT, w_words, w_scales, gate, offs, pos1, pos2, ou
         wp0 = weave(False, sgring, "grs", p0)
         gather(False, p1, (2, 3))
 
-        wd0 = weave(True, vring, "grv", previous[0])
-        multiply(w3[0])
-        wd1 = weave(True, vring, "grv", previous[1])
-        multiply(w3[1])
-        multiply(wd0)
-        multiply(w3[2])
-        multiply(wd1)
-        multiply(w3[3])
+        gd = vector_group(1, high)
+        group_gather(gd, (0, 1))
+        wc = group_weave(gc)
+        multiply(w30)
+        multiply(w31)
+        w32 = weave(True, sgring, "grs", s3[2])
+        w33 = weave(True, sgring, "grs", s3[3])
+        group_gather(gd, (2, 3))
+        multiply(wc[0])
+        multiply(wc[1])
+        multiply(w32)
+        multiply(w33)
+        multiply(wp0)
 
         p2 = start(suring, "us", 2, (4, 5))
         gather(False, p2, (0, 1))
@@ -193,22 +202,24 @@ def tile_routed_moe_kernel(tc, xT, w_words, w_scales, gate, offs, pos1, pos2, ou
         gather(False, p3a, (0, 1))
         wp2 = weave(False, sgring, "grs", p2)
         gather(False, p3a, (2, 3))
+        take_out(False, 0)
+        take_out(False, 1)
         p3b = start(suring, "us", 2, (7,))
         gather(False, p3b, (0, 1))
         wp3a = weave(False, sgring, "grs", p3a)
         gather(False, p3b, (2, 3))
         wp3b = weave(False, sgring, "grs", p3b)
 
-        multiply(wp0)
+        wd = group_weave(gd)
         multiply(wp1)
+        multiply(wd[0])
+        multiply(wd[1])
         multiply(wp2)
-        for e in range(0, 4):
-            take_out(True, e)
-        for e in range(4, 6):
+        for e in range(2, 6):
             take_out(False, e)
         multiply(wp3a)
-        take_out(False, 6)
         multiply(wp3b)
+        take_out(True, 6)
         take_out(True, 7)
 
         for h in range(T // HALF):

@@ -30,7 +30,8 @@ def tile_routed_moe_kernel(tc, xT, w_words, w_scales, gate, offs, pos1, pos2, ou
         lists = ctx.enter_context(tc.tile_pool(name="lists", bufs=1))
         keep = ctx.enter_context(tc.tile_pool(name="keep", bufs=1))
         stage = ctx.enter_context(tc.tile_pool(name="stage", bufs=5))
-        vring = ctx.enter_context(tc.tile_pool(name="vring", bufs=4))
+        vuring = ctx.enter_context(tc.tile_pool(name="vuring", bufs=6))
+        vgring = ctx.enter_context(tc.tile_pool(name="vgring", bufs=4))
         suring = ctx.enter_context(tc.tile_pool(name="suring", bufs=6))
         sgring = ctx.enter_context(tc.tile_pool(name="sgring", bufs=7))
         qring = ctx.enter_context(tc.tile_pool(name="qring", bufs=8))
@@ -59,8 +60,11 @@ def tile_routed_moe_kernel(tc, xT, w_words, w_scales, gate, offs, pos1, pos2, ou
             nc.sync.dma_start(st[:], x_view[g, :, t, :])
             staged[(g, t)] = st
 
-        def cast(g, t):
-            nc.scalar.copy(xb[g][:, t, :], staged[(g, t)][:])
+        def cast(on_scalar, g, t):
+            if on_scalar:
+                nc.scalar.copy(xb[g][:, t, :], staged[(g, t)][:])
+            else:
+                nc.gpsimd.tensor_copy(xb[g][:, t, :], staged[(g, t)][:])
 
         def start(pool, tag, g, experts):
             u = pool.tile([P, PACK * C * len(experts)], BF16, name=tag)
@@ -113,20 +117,24 @@ def tile_routed_moe_kernel(tc, xT, w_words, w_scales, gate, offs, pos1, pos2, ou
                 nc.scalar.copy(y[:, e * C : (e + 1) * C], acc[e][:])
 
         def vector_group(g, pairs):
-            return [start(vring, "uv", g, experts) for experts in pairs]
+            return [start(vuring, "uv", g, experts) for experts in pairs]
 
         def group_gather(group, planes):
             for t in planes:
                 for piece in group:
                     gather(True, piece, (t,))
 
-        def group_weave(group):
-            return [weave(True, vring, "grv", piece) for piece in group]
+        def vweave(piece):
+            return weave(True, vgring, "grv", piece)
+
+        def sweave(piece):
+            return weave(False, sgring, "grs", piece)
 
         nc.vector.memset(w_planes[:].bitcast(I32), 0)
         for t in range(PACK):
             nc.sync.dma_start(raw[0][:, t, :], x_view[0, :, t, :])
             load_staged(3, t)
+        load_staged(2, 0)
         for t in range(PACK):
             nc.sync.dma_start(raw[1][:, t, :], x_view[1, :, t, :])
 
@@ -136,11 +144,11 @@ def tile_routed_moe_kernel(tc, xT, w_words, w_scales, gate, offs, pos1, pos2, ou
 
         s3 = [start(suring, "us", 3, experts) for experts in low + high]
         for t in range(PACK):
-            cast(3, t)
+            cast(t == 0, 3, t)
             for piece in s3:
                 gather(False, piece, (t,))
 
-        for t in range(PACK):
+        for t in (1, 2, 3):
             load_staged(2, t)
         for a in range(PASSES):
             for r in range(4):
@@ -154,66 +162,68 @@ def tile_routed_moe_kernel(tc, xT, w_words, w_scales, gate, offs, pos1, pos2, ou
         nc.sync.dma_start(pos2_t[:], pos2)
         nc.sync.dma_start(gate_t[:], gate.rearrange("r n t -> n r t"))
 
+        cast(False, 2, 0)
+
         gb = vector_group(0, high)
-        group_gather(gb, (0, 1))
-        wa = group_weave(ga)
-        group_gather(gb, (2, 3))
-        multiply(wa[0])
-        multiply(wa[1])
-
-        for t in range(PACK):
-            cast(2, t)
-
+        group_gather(gb, range(PACK))
         gc = vector_group(1, low)
-        group_gather(gc, (0, 1))
-        wb = group_weave(gb)
-        group_gather(gc, (2, 3))
-        multiply(wb[0])
-        multiply(wb[1])
-        w30 = weave(True, sgring, "grs", s3[0])
-        w31 = weave(True, sgring, "grs", s3[1])
+        group_gather(gc, range(PACK))
+
+        w3 = [sweave(piece) for piece in s3[:3]]
+        for t in (1, 2, 3):
+            cast(True, 2, t)
+
+        wa0 = vweave(ga[0])
+        wa1 = vweave(ga[1])
+        wb0 = vweave(gb[0])
+        multiply(wa0)
+        wb1 = vweave(gb[1])
+        multiply(wa1)
 
         p0 = start(suring, "us", 2, (0, 1))
         gather(False, p0, range(PACK))
         p1 = start(suring, "us", 2, (2, 3))
         gather(False, p1, (0, 1))
-        wp0 = weave(False, sgring, "grs", p0)
+        wp0 = sweave(p0)
         gather(False, p1, (2, 3))
 
         gd = vector_group(1, high)
         group_gather(gd, (0, 1))
-        wc = group_weave(gc)
-        multiply(w30)
-        multiply(w31)
-        w32 = weave(True, sgring, "grs", s3[2])
-        w33 = weave(True, sgring, "grs", s3[3])
+        multiply(wb0)
+        multiply(wb1)
+        wc0 = vweave(gc[0])
+        wc1 = vweave(gc[1])
+        w3.append(weave(True, sgring, "grs", s3[3]))
+        multiply(w3[0])
+        multiply(w3[1])
         group_gather(gd, (2, 3))
-        multiply(wc[0])
-        multiply(wc[1])
-        multiply(w32)
-        multiply(w33)
+        multiply(wc0)
+        multiply(wc1)
+        multiply(w3[2])
+        multiply(w3[3])
         multiply(wp0)
 
         p2 = start(suring, "us", 2, (4, 5))
         gather(False, p2, (0, 1))
-        wp1 = weave(False, sgring, "grs", p1)
+        wp1 = sweave(p1)
         gather(False, p2, (2, 3))
         p3a = start(suring, "us", 2, (6,))
         gather(False, p3a, (0, 1))
-        wp2 = weave(False, sgring, "grs", p2)
+        wp2 = sweave(p2)
         gather(False, p3a, (2, 3))
         take_out(False, 0)
         take_out(False, 1)
         p3b = start(suring, "us", 2, (7,))
         gather(False, p3b, (0, 1))
-        wp3a = weave(False, sgring, "grs", p3a)
+        wp3a = sweave(p3a)
         gather(False, p3b, (2, 3))
-        wp3b = weave(False, sgring, "grs", p3b)
+        wp3b = sweave(p3b)
 
-        wd = group_weave(gd)
+        wd0 = vweave(gd[0])
+        wd1 = vweave(gd[1])
         multiply(wp1)
-        multiply(wd[0])
-        multiply(wd[1])
+        multiply(wd0)
+        multiply(wd1)
         multiply(wp2)
         for e in range(2, 6):
             take_out(False, e)

@@ -22,6 +22,7 @@ SLOTS = E * C
 HALF = 512
 LIST_COLS = C // 16
 FIRST_PASS, LAST_PASS = 0, 2
+PAIRS = ((0, 1), (2, 3), (4, 5), (6, 7))
 
 
 def tile_routed_moe_kernel(tc, xT, w_words, w_scales, gate, offs, pos1, pos2, out):
@@ -29,12 +30,11 @@ def tile_routed_moe_kernel(tc, xT, w_words, w_scales, gate, offs, pos1, pos2, ou
     with ExitStack() as ctx:
         lists = ctx.enter_context(tc.tile_pool(name="lists", bufs=1))
         keep = ctx.enter_context(tc.tile_pool(name="keep", bufs=1))
-        stage = ctx.enter_context(tc.tile_pool(name="stage", bufs=5))
-        vuring = ctx.enter_context(tc.tile_pool(name="vuring", bufs=6))
-        vgring = ctx.enter_context(tc.tile_pool(name="vgring", bufs=4))
-        suring = ctx.enter_context(tc.tile_pool(name="suring", bufs=6))
-        sgring = ctx.enter_context(tc.tile_pool(name="sgring", bufs=7))
-        qring = ctx.enter_context(tc.tile_pool(name="qring", bufs=8))
+        stage = ctx.enter_context(tc.tile_pool(name="stage", bufs=4))
+        vuring = ctx.enter_context(tc.tile_pool(name="vuring", bufs=4))
+        suring = ctx.enter_context(tc.tile_pool(name="suring", bufs=4))
+        woven = ctx.enter_context(tc.tile_pool(name="woven", bufs=1))
+        qring = ctx.enter_context(tc.tile_pool(name="qring", bufs=4))
         tail = ctx.enter_context(tc.tile_pool(name="tail", bufs=2))
         psum = ctx.enter_context(tc.psum_pool(name="psum", bufs=1))
 
@@ -60,13 +60,11 @@ def tile_routed_moe_kernel(tc, xT, w_words, w_scales, gate, offs, pos1, pos2, ou
             nc.sync.dma_start(st[:], x_view[g, :, t, :])
             staged[(g, t)] = st
 
-        def cast(on_scalar, g, t):
-            if on_scalar:
-                nc.scalar.copy(xb[g][:, t, :], staged[(g, t)][:])
-            else:
-                nc.gpsimd.tensor_copy(xb[g][:, t, :], staged[(g, t)][:])
+        def cast(g, t):
+            nc.gpsimd.tensor_copy(xb[g][:, t, :], staged[(g, t)][:])
 
-        def start(pool, tag, g, experts):
+        def start(on_vector, g, experts):
+            pool, tag = (vuring, "uv") if on_vector else (suring, "us")
             u = pool.tile([P, PACK * C * len(experts)], BF16, name=tag)
             return (g, experts, u)
 
@@ -82,19 +80,16 @@ def tile_routed_moe_kernel(tc, xT, w_words, w_scales, gate, offs, pos1, pos2, ou
                     else:
                         nc.scalar.activation(dst, xb[g][:, t, :].indirect(lst), COPY)
 
-        def weave(on_vector, pool, tag, piece):
+        def weave(engine, piece):
             g, experts, u = piece
-            gr = pool.tile([P, PACK * C * len(experts)], BF16, name=tag, align_bytes=64)
+            gr = woven.tile([P, PACK * C * len(experts)], BF16, name="gr%d_%d" % (g, experts[0]), align_bytes=64)
             dst = gr[:].bitcast(F32).rearrange("p (n h) -> p n h", h=2)
             src = u[:].bitcast(F32).rearrange("p (h n) -> p n h", h=2)
-            if on_vector:
-                nc.vector.tensor_copy(dst, src)
-            else:
-                nc.scalar.copy(dst, src)
+            engine.tensor_copy(dst, src)
             return (g, experts, gr)
 
-        def multiply(woven):
-            g, experts, gr = woven
+        def multiply(piece):
+            g, experts, gr = piece
             n = C * len(experts)
             codes = qring.tile([P, n], I32, name="codes", align_bytes=64)
             scales = qring.tile([P, n], U8, name="scales", align_bytes=64)
@@ -116,39 +111,23 @@ def tile_routed_moe_kernel(tc, xT, w_words, w_scales, gate, offs, pos1, pos2, ou
             else:
                 nc.scalar.copy(y[:, e * C : (e + 1) * C], acc[e][:])
 
-        def vector_group(g, pairs):
-            return [start(vuring, "uv", g, experts) for experts in pairs]
-
-        def group_gather(group, planes):
-            for t in planes:
-                for piece in group:
-                    gather(True, piece, (t,))
-
-        def vweave(piece):
-            return weave(True, vgring, "grv", piece)
-
-        def sweave(piece):
-            return weave(False, sgring, "grs", piece)
-
         nc.vector.memset(w_planes[:].bitcast(I32), 0)
         for t in range(PACK):
             nc.sync.dma_start(raw[0][:, t, :], x_view[0, :, t, :])
             load_staged(3, t)
-        load_staged(2, 0)
+
+        done = {}
+
+        va = [start(True, 0, PAIRS[0]), start(True, 0, PAIRS[1])]
+        sa = [start(False, 3, PAIRS[0]), start(False, 3, PAIRS[1])]
+        for t in range(PACK):
+            cast(3, t)
+            for piece in va:
+                gather(True, piece, (t,))
+            for piece in sa:
+                gather(False, piece, (t,))
         for t in range(PACK):
             nc.sync.dma_start(raw[1][:, t, :], x_view[1, :, t, :])
-
-        low, high = ((0, 1), (2, 3)), ((4, 5), (6, 7))
-        ga = vector_group(0, low)
-        group_gather(ga, range(PACK))
-
-        s3 = [start(suring, "us", 3, experts) for experts in low + high]
-        for t in range(PACK):
-            cast(t == 0, 3, t)
-            for piece in s3:
-                gather(False, piece, (t,))
-
-        for t in (1, 2, 3):
             load_staged(2, t)
         for a in range(PASSES):
             for r in range(4):
@@ -162,74 +141,43 @@ def tile_routed_moe_kernel(tc, xT, w_words, w_scales, gate, offs, pos1, pos2, ou
         nc.sync.dma_start(pos2_t[:], pos2)
         nc.sync.dma_start(gate_t[:], gate.rearrange("r n t -> n r t"))
 
-        cast(False, 2, 0)
+        for piece in va + sa:
+            done[(piece[0], piece[1][0])] = weave(nc.gpsimd, piece)
 
-        gb = vector_group(0, high)
-        group_gather(gb, range(PACK))
-        gc = vector_group(1, low)
-        group_gather(gc, range(PACK))
+        steps = [((0, 2), (3, 2)), ((0, 3), (3, 3)), ((1, 0), (2, 0)), ((1, 1), (2, 1)), ((1, 2), (2, 2))]
+        for i, (vp, sp) in enumerate(steps):
+            if i < 2:
+                cast(2, 2 * i)
+                cast(2, 2 * i + 1)
+            pv = start(True, vp[0], PAIRS[vp[1]])
+            gather(True, pv, range(PACK))
+            ps = start(False, sp[0], PAIRS[sp[1]])
+            gather(False, ps, range(PACK))
+            done[(pv[0], pv[1][0])] = weave(nc.gpsimd, pv)
+            done[(ps[0], ps[1][0])] = weave(nc.gpsimd, ps)
 
-        w3 = [sweave(piece) for piece in s3[:3]]
-        for t in (1, 2, 3):
-            cast(True, 2, t)
+        pv = start(True, 1, PAIRS[3])
+        gather(True, pv, range(PACK))
+        p6 = start(False, 2, (6,))
+        gather(False, p6, range(PACK))
+        p7 = start(False, 2, (7,))
+        gather(False, p7, range(PACK))
 
-        wa0 = vweave(ga[0])
-        wa1 = vweave(ga[1])
-        wb0 = vweave(gb[0])
-        multiply(wa0)
-        wb1 = vweave(gb[1])
-        multiply(wa1)
-
-        p0 = start(suring, "us", 2, (0, 1))
-        gather(False, p0, range(PACK))
-        p1 = start(suring, "us", 2, (2, 3))
-        gather(False, p1, (0, 1))
-        wp0 = sweave(p0)
-        gather(False, p1, (2, 3))
-
-        gd = vector_group(1, high)
-        group_gather(gd, (0, 1))
-        multiply(wb0)
-        multiply(wb1)
-        wc0 = vweave(gc[0])
-        wc1 = vweave(gc[1])
-        w3.append(weave(True, sgring, "grs", s3[3]))
-        multiply(w3[0])
-        multiply(w3[1])
-        group_gather(gd, (2, 3))
-        multiply(wc0)
-        multiply(wc1)
-        multiply(w3[2])
-        multiply(w3[3])
-        multiply(wp0)
-
-        p2 = start(suring, "us", 2, (4, 5))
-        gather(False, p2, (0, 1))
-        wp1 = sweave(p1)
-        gather(False, p2, (2, 3))
-        p3a = start(suring, "us", 2, (6,))
-        gather(False, p3a, (0, 1))
-        wp2 = sweave(p2)
-        gather(False, p3a, (2, 3))
-        take_out(False, 0)
-        take_out(False, 1)
-        p3b = start(suring, "us", 2, (7,))
-        gather(False, p3b, (0, 1))
-        wp3a = sweave(p3a)
-        gather(False, p3b, (2, 3))
-        wp3b = sweave(p3b)
-
-        wd0 = vweave(gd[0])
-        wd1 = vweave(gd[1])
-        multiply(wp1)
-        multiply(wd0)
-        multiply(wd1)
-        multiply(wp2)
-        for e in range(2, 6):
-            take_out(False, e)
-        multiply(wp3a)
-        multiply(wp3b)
-        take_out(True, 6)
+        done[(1, 6)] = weave(nc.vector, pv)
+        for g in (0, 3):
+            for pair in PAIRS:
+                multiply(done[(g, pair[0])])
+        w6 = weave(nc.vector, p6)
+        for pair in PAIRS:
+            multiply(done[(1, pair[0])])
+        w7 = weave(nc.vector, p7)
+        for pair in PAIRS[:3]:
+            multiply(done[(2, pair[0])])
+            take_out(False, pair[0])
+            take_out(False, pair[1])
+        multiply(w6)
+        multiply(w7)
+        take_out(False, 6)
         take_out(True, 7)
 
         for h in range(T // HALF):

@@ -30,10 +30,10 @@ def tile_routed_moe_kernel(tc, xT, w_words, w_scales, gate, offs, pos1, pos2, ou
     with ExitStack() as ctx:
         lists = ctx.enter_context(tc.tile_pool(name="lists", bufs=1))
         keep = ctx.enter_context(tc.tile_pool(name="keep", bufs=1))
-        stage = ctx.enter_context(tc.tile_pool(name="stage", bufs=4))
-        vuring = ctx.enter_context(tc.tile_pool(name="vuring", bufs=4))
-        suring = ctx.enter_context(tc.tile_pool(name="suring", bufs=4))
-        woven = ctx.enter_context(tc.tile_pool(name="woven", bufs=1))
+        stage = ctx.enter_context(tc.tile_pool(name="stage", bufs=8))
+        vuring = ctx.enter_context(tc.tile_pool(name="vuring", bufs=2))
+        suring = ctx.enter_context(tc.tile_pool(name="suring", bufs=2))
+        woven = ctx.enter_context(tc.tile_pool(name="woven", bufs=4))
         qring = ctx.enter_context(tc.tile_pool(name="qring", bufs=4))
         tail = ctx.enter_context(tc.tile_pool(name="tail", bufs=2))
         psum = ctx.enter_context(tc.psum_pool(name="psum", bufs=1))
@@ -82,7 +82,7 @@ def tile_routed_moe_kernel(tc, xT, w_words, w_scales, gate, offs, pos1, pos2, ou
 
         def weave(engine, piece):
             g, experts, u = piece
-            gr = woven.tile([P, PACK * C * len(experts)], BF16, name="gr%d_%d" % (g, experts[0]), align_bytes=64)
+            gr = woven.tile([P, PACK * C * len(experts)], BF16, name="gr", align_bytes=64)
             dst = gr[:].bitcast(F32).rearrange("p (n h) -> p n h", h=2)
             src = u[:].bitcast(F32).rearrange("p (h n) -> p n h", h=2)
             engine.tensor_copy(dst, src)
@@ -115,19 +115,9 @@ def tile_routed_moe_kernel(tc, xT, w_words, w_scales, gate, offs, pos1, pos2, ou
         for t in range(PACK):
             nc.sync.dma_start(raw[0][:, t, :], x_view[0, :, t, :])
             load_staged(3, t)
-
-        done = {}
-
-        va = [start(True, 0, PAIRS[0]), start(True, 0, PAIRS[1])]
-        sa = [start(False, 3, PAIRS[0]), start(False, 3, PAIRS[1])]
-        for t in range(PACK):
-            cast(3, t)
-            for piece in va:
-                gather(True, piece, (t,))
-            for piece in sa:
-                gather(False, piece, (t,))
         for t in range(PACK):
             nc.sync.dma_start(raw[1][:, t, :], x_view[1, :, t, :])
+        for t in range(PACK):
             load_staged(2, t)
         for a in range(PASSES):
             for r in range(4):
@@ -141,42 +131,42 @@ def tile_routed_moe_kernel(tc, xT, w_words, w_scales, gate, offs, pos1, pos2, ou
         nc.sync.dma_start(pos2_t[:], pos2)
         nc.sync.dma_start(gate_t[:], gate.rearrange("r n t -> n r t"))
 
-        for piece in va + sa:
-            done[(piece[0], piece[1][0])] = weave(nc.gpsimd, piece)
-
-        steps = [((0, 2), (3, 2)), ((0, 3), (3, 3)), ((1, 0), (2, 0)), ((1, 1), (2, 1)), ((1, 2), (2, 2))]
-        for i, (vp, sp) in enumerate(steps):
-            if i < 2:
-                cast(2, 2 * i)
-                cast(2, 2 * i + 1)
-            pv = start(True, vp[0], PAIRS[vp[1]])
-            gather(True, pv, range(PACK))
-            ps = start(False, sp[0], PAIRS[sp[1]])
-            gather(False, ps, range(PACK))
-            done[(pv[0], pv[1][0])] = weave(nc.gpsimd, pv)
-            done[(ps[0], ps[1][0])] = weave(nc.gpsimd, ps)
-
-        pv = start(True, 1, PAIRS[3])
-        gather(True, pv, range(PACK))
-        p6 = start(False, 2, (6,))
-        gather(False, p6, range(PACK))
-        p7 = start(False, 2, (7,))
-        gather(False, p7, range(PACK))
-
-        done[(1, 6)] = weave(nc.vector, pv)
-        for g in (0, 3):
-            for pair in PAIRS:
-                multiply(done[(g, pair[0])])
-        w6 = weave(nc.vector, p6)
-        for pair in PAIRS:
-            multiply(done[(1, pair[0])])
-        w7 = weave(nc.vector, p7)
-        for pair in PAIRS[:3]:
-            multiply(done[(2, pair[0])])
-            take_out(False, pair[0])
-            take_out(False, pair[1])
-        multiply(w6)
-        multiply(w7)
+        vorder = [(0, 0), (0, 1), (0, 2), (0, 3), (1, 0), (1, 1), (1, 2), (1, 3)]
+        sorder = [(3, 0), (3, 1), (3, 2), (3, 3), (2, 0), (2, 1), (2, 2), (2, 3)]
+        vp = {}
+        sp = {}
+        wv = {}
+        ws = {}
+        for k in (0, 1):
+            vp[k] = start(True, vorder[k][0], PAIRS[vorder[k][1]])
+            sp[k] = start(False, sorder[k][0], PAIRS[sorder[k][1]])
+        for t in range(PACK):
+            cast(3, t)
+            for k in (0, 1):
+                gather(True, vp[k], (t,))
+            for k in (0, 1):
+                gather(False, sp[k], (t,))
+        for k in (0, 1):
+            wv[k] = weave(nc.gpsimd, vp[k])
+        for k in (0, 1):
+            ws[k] = weave(nc.gpsimd, sp[k])
+        for t in range(PACK):
+            cast(2, t)
+        for k in range(2, 8):
+            vp[k] = start(True, vorder[k][0], PAIRS[vorder[k][1]])
+            gather(True, vp[k], range(PACK))
+            sp[k] = start(False, sorder[k][0], PAIRS[sorder[k][1]])
+            gather(False, sp[k], range(PACK))
+            multiply(wv[k - 2])
+            multiply(ws[k - 2])
+            wv[k] = weave(nc.gpsimd if k < 8 - 2 + 1 else nc.vector, vp[k])
+            ws[k] = weave(nc.gpsimd if k < 8 - 2 + 1 else nc.vector, sp[k])
+        multiply(wv[6])
+        multiply(ws[6])
+        for e in range(6):
+            take_out(False, e)
+        multiply(wv[7])
+        multiply(ws[7])
         take_out(False, 6)
         take_out(True, 7)
 

@@ -31,10 +31,10 @@ def tile_routed_moe_kernel(tc, xT, w_words, w_scales, gate, offs, pos1, pos2, ou
         lists = ctx.enter_context(tc.tile_pool(name="lists", bufs=1))
         keep = ctx.enter_context(tc.tile_pool(name="keep", bufs=1))
         stage = ctx.enter_context(tc.tile_pool(name="stage", bufs=8))
-        vuring = ctx.enter_context(tc.tile_pool(name="vuring", bufs=2))
-        suring = ctx.enter_context(tc.tile_pool(name="suring", bufs=2))
-        woven = ctx.enter_context(tc.tile_pool(name="woven", bufs=4))
-        qring = ctx.enter_context(tc.tile_pool(name="qring", bufs=4))
+        vuring = ctx.enter_context(tc.tile_pool(name="vuring", bufs=3))
+        suring = ctx.enter_context(tc.tile_pool(name="suring", bufs=3))
+        woven = ctx.enter_context(tc.tile_pool(name="woven", bufs=6))
+        qring = ctx.enter_context(tc.tile_pool(name="qring", bufs=6))
         tail = ctx.enter_context(tc.tile_pool(name="tail", bufs=2))
         psum = ctx.enter_context(tc.psum_pool(name="psum", bufs=1))
 
@@ -85,7 +85,12 @@ def tile_routed_moe_kernel(tc, xT, w_words, w_scales, gate, offs, pos1, pos2, ou
             gr = woven.tile([P, PACK * C * len(experts)], BF16, name="gr", align_bytes=64)
             dst = gr[:].bitcast(F32).rearrange("p (n h) -> p n h", h=2)
             src = u[:].bitcast(F32).rearrange("p (h n) -> p n h", h=2)
-            engine.tensor_copy(dst, src)
+            if engine == "S":
+                nc.scalar.copy(dst, src)
+            elif engine == "V":
+                nc.vector.tensor_copy(dst, src)
+            else:
+                nc.gpsimd.tensor_copy(dst, src)
             return (g, experts, gr)
 
         def multiply(piece):
@@ -146,28 +151,46 @@ def tile_routed_moe_kernel(tc, xT, w_words, w_scales, gate, offs, pos1, pos2, ou
                 gather(True, vp[k], (t,))
             for k in (0, 1):
                 gather(False, sp[k], (t,))
+        s_self = ()
+        v_self = ()
         for k in (0, 1):
-            wv[k] = weave(nc.gpsimd, vp[k])
+            wv[k] = weave("V" if k in v_self else "G", vp[k])
         for k in (0, 1):
-            ws[k] = weave(nc.gpsimd, sp[k])
+            ws[k] = weave("S" if k in s_self else "G", sp[k])
         for t in range(PACK):
             cast(2, t)
-        for k in range(2, 8):
+        for k in range(2, 7):
             vp[k] = start(True, vorder[k][0], PAIRS[vorder[k][1]])
-            gather(True, vp[k], range(PACK))
             sp[k] = start(False, sorder[k][0], PAIRS[sorder[k][1]])
+            gather(True, vp[k], range(PACK))
             gather(False, sp[k], range(PACK))
             multiply(wv[k - 2])
             multiply(ws[k - 2])
-            wv[k] = weave(nc.gpsimd if k < 8 - 2 + 1 else nc.vector, vp[k])
-            ws[k] = weave(nc.gpsimd if k < 8 - 2 + 1 else nc.vector, sp[k])
+            wv[k] = weave("V" if k in v_self else "G", vp[k])
+            ws[k] = weave("S" if k in s_self else "G", sp[k])
+        v7a = start(True, 1, (6,))
+        gather(True, v7a, range(PACK))
+        s7a = start(False, 2, (6,))
+        gather(False, s7a, range(PACK))
+        v7b = start(True, 1, (7,))
+        gather(True, v7b, range(PACK))
+        s7b = start(False, 2, (7,))
+        gather(False, s7b, range(PACK))
+        multiply(wv[5])
+        multiply(ws[5])
+        wva = weave("V", v7a)
         multiply(wv[6])
+        wsa = weave("V", s7a)
         multiply(ws[6])
+        multiply(wva)
+        wvb = weave("V", v7b)
+        multiply(wsa)
+        wsb = weave("V", s7b)
         for e in range(6):
             take_out(False, e)
-        multiply(wv[7])
-        multiply(ws[7])
+        multiply(wvb)
         take_out(False, 6)
+        multiply(wsb)
         take_out(True, 7)
 
         for h in range(T // HALF):

@@ -21,8 +21,11 @@ PASSES = K // (P * PACK)
 SLOTS = E * C
 HALF = 512
 LIST_COLS = C // 16
-FIRST_PASS, LAST_PASS = 0, 2
-PAIRS = ((0, 1), (2, 3), (4, 5), (6, 7))
+LOW = (0, 1, 2, 3)
+HIGH = (4, 5, 6, 7)
+SHARED = (4, 5, 6, 7)
+TAIL_PIECES = ((4, 5), (6,), (7,))
+V_OUT = (4, 5, 6)
 
 
 def tile_routed_moe_kernel(tc, xT, w_words, w_scales, gate, offs, pos1, pos2, out):
@@ -30,11 +33,8 @@ def tile_routed_moe_kernel(tc, xT, w_words, w_scales, gate, offs, pos1, pos2, ou
     with ExitStack() as ctx:
         lists = ctx.enter_context(tc.tile_pool(name="lists", bufs=1))
         keep = ctx.enter_context(tc.tile_pool(name="keep", bufs=1))
-        stage = ctx.enter_context(tc.tile_pool(name="stage", bufs=8))
-        vuring = ctx.enter_context(tc.tile_pool(name="vuring", bufs=3))
-        suring = ctx.enter_context(tc.tile_pool(name="suring", bufs=3))
-        woven = ctx.enter_context(tc.tile_pool(name="woven", bufs=6))
-        qring = ctx.enter_context(tc.tile_pool(name="qring", bufs=6))
+        woven = ctx.enter_context(tc.tile_pool(name="woven", bufs=3))
+        qring = ctx.enter_context(tc.tile_pool(name="qring", bufs=3))
         tail = ctx.enter_context(tc.tile_pool(name="tail", bufs=2))
         psum = ctx.enter_context(tc.psum_pool(name="psum", bufs=1))
 
@@ -45,8 +45,11 @@ def tile_routed_moe_kernel(tc, xT, w_words, w_scales, gate, offs, pos1, pos2, ou
 
         x_view = xT.rearrange("(g p t) n -> g p t n", p=P, t=PACK)
         raw = dict((g, keep.tile([P, PACK, T], F32, name="raw%d" % g)) for g in (0, 1))
-        xb = dict((g, keep.tile([P, PACK, T], BF16, name="xb%d" % g)) for g in (3, 2))
-        staged = {}
+        xb3 = keep.tile([P, PACK, T], BF16, name="xb3")
+        xb2 = keep.tile([P, PACK, T], BF16, name="xb2")
+        xb1 = keep.tile([P, 2, T], BF16, name="xb1")
+        st3 = [keep.tile([P, 2, T], F32, name="slot_a"), keep.tile([P, 2, T], F32, name="slot_b")]
+        st2 = [keep.tile([P, 2, T], F32, name="slot_c", align_bytes=64), keep.tile([P, 2, T], F32, name="slot_d", align_bytes=64)]
         w_codes = keep.tile([P, PASSES, E, N], I32, name="w_codes", align_bytes=64)
         w_planes = keep.tile([P, E * N], U8, name="w_planes", align_bytes=64)
         w_view = w_words.rearrange("e a p n r -> a p e (n r)")
@@ -55,34 +58,31 @@ def tile_routed_moe_kernel(tc, xT, w_words, w_scales, gate, offs, pos1, pos2, ou
         acc = [psum.tile([P, C], F32, name="acc%d" % e) for e in range(E)]
         y = keep.tile([P, SLOTS], F32, name="y")
 
-        def load_staged(g, t):
-            st = stage.tile([P, T], F32, name="st")
-            nc.sync.dma_start(st[:], x_view[g, :, t, :])
-            staged[(g, t)] = st
-
-        def cast(g, t):
-            nc.gpsimd.tensor_copy(xb[g][:, t, :], staged[(g, t)][:])
-
-        def start(on_vector, g, experts):
-            pool, tag = (vuring, "uv") if on_vector else (suring, "us")
-            u = pool.tile([P, PACK * C * len(experts)], BF16, name=tag)
+        def piece(name, g, experts):
+            u = keep.tile([P, PACK * C * len(experts)], BF16, name=name)
             return (g, experts, u)
 
-        def gather(on_vector, piece, planes):
-            g, experts, u = piece
+        def gather(on_vector, pc, planes, only=None):
+            g, experts, u = pc
             view = u[:].rearrange("p (h n e) -> p h n e", h=2, e=2)
             for t in planes:
                 for j, e in enumerate(experts):
+                    if only is not None and e not in only:
+                        continue
                     dst = view[:, t // 2, j * C : (j + 1) * C, t % 2]
                     lst = offs_t[:, e * LIST_COLS : (e + 1) * LIST_COLS]
                     if on_vector:
                         nc.vector.tensor_copy(dst, raw[g][:, t, :].indirect(lst))
                     else:
-                        nc.scalar.activation(dst, xb[g][:, t, :].indirect(lst), COPY)
+                        window = xb3[:, t, :] if g == 3 else (xb2[:, t, :] if g == 2 else xb1[:, t - 2, :])
+                        nc.scalar.activation(dst, window.indirect(lst), COPY)
 
-        def weave(engine, piece):
-            g, experts, u = piece
-            gr = woven.tile([P, PACK * C * len(experts)], BF16, name="gr", align_bytes=64)
+        def weave(engine, pc, slot=None):
+            g, experts, u = pc
+            if slot is None:
+                gr = woven.tile([P, PACK * C * len(experts)], BF16, name="gr", align_bytes=64)
+            else:
+                gr = keep.tile([P, PACK * C * len(experts)], BF16, name=slot, align_bytes=64)
             dst = gr[:].bitcast(F32).rearrange("p (n h) -> p n h", h=2)
             src = u[:].bitcast(F32).rearrange("p (h n) -> p n h", h=2)
             if engine == "S":
@@ -93,8 +93,8 @@ def tile_routed_moe_kernel(tc, xT, w_words, w_scales, gate, offs, pos1, pos2, ou
                 nc.gpsimd.tensor_copy(dst, src)
             return (g, experts, gr)
 
-        def multiply(piece):
-            g, experts, gr = piece
+        def multiply(pc):
+            g, experts, gr = pc
             n = C * len(experts)
             codes = qring.tile([P, n], I32, name="codes", align_bytes=64)
             scales = qring.tile([P, n], U8, name="scales", align_bytes=64)
@@ -106,12 +106,12 @@ def tile_routed_moe_kernel(tc, xT, w_words, w_scales, gate, offs, pos1, pos2, ou
                     lhsT_scale=w_planes[4 * g : P, e * N : (e + 1) * N],
                     rhs=codes[:, j * C : (j + 1) * C].bitcast(FP8X4),
                     rhs_scale=scales[:, j * C : (j + 1) * C],
-                    start=(g == FIRST_PASS),
-                    stop=(g == LAST_PASS),
+                    start=(g == 0),
+                    stop=(g == (2 if e in LOW else 1)),
                 )
 
-        def take_out(on_vector, e):
-            if on_vector:
+        def take_out(e):
+            if e in V_OUT:
                 nc.vector.tensor_copy(y[:, e * C : (e + 1) * C], acc[e][:])
             else:
                 nc.scalar.copy(y[:, e * C : (e + 1) * C], acc[e][:])
@@ -119,11 +119,11 @@ def tile_routed_moe_kernel(tc, xT, w_words, w_scales, gate, offs, pos1, pos2, ou
         nc.vector.memset(w_planes[:].bitcast(I32), 0)
         for t in range(PACK):
             nc.sync.dma_start(raw[0][:, t, :], x_view[0, :, t, :])
-            load_staged(3, t)
+            nc.sync.dma_start(st3[t // 2][:, t % 2, :], x_view[3, :, t, :])
         for t in range(PACK):
+            nc.sync.dma_start(st2[t // 2][:, t % 2, :], x_view[2, :, t, :])
+        for t in (2, 3, 0, 1):
             nc.sync.dma_start(raw[1][:, t, :], x_view[1, :, t, :])
-        for t in range(PACK):
-            load_staged(2, t)
         for a in range(PASSES):
             for r in range(4):
                 nc.sync.dma_start(
@@ -136,62 +136,50 @@ def tile_routed_moe_kernel(tc, xT, w_words, w_scales, gate, offs, pos1, pos2, ou
         nc.sync.dma_start(pos2_t[:], pos2)
         nc.sync.dma_start(gate_t[:], gate.rearrange("r n t -> n r t"))
 
-        vorder = [(0, 0), (0, 1), (0, 2), (0, 3), (1, 0), (1, 1), (1, 2), (1, 3)]
-        sorder = [(3, 0), (3, 1), (3, 2), (3, 3), (2, 0), (2, 1), (2, 2), (2, 3)]
-        vp = {}
-        sp = {}
-        wv = {}
-        ws = {}
-        for k in (0, 1):
-            vp[k] = start(True, vorder[k][0], PAIRS[vorder[k][1]])
-            sp[k] = start(False, sorder[k][0], PAIRS[sorder[k][1]])
+        va = [piece("va0", 0, LOW), piece("va1", 0, HIGH)]
+        sa = [piece("sa0", 3, LOW), piece("sa1", 3, HIGH)]
         for t in range(PACK):
-            cast(3, t)
-            for k in (0, 1):
-                gather(True, vp[k], (t,))
-            for k in (0, 1):
-                gather(False, sp[k], (t,))
-        s_self = ()
-        v_self = ()
-        for k in (0, 1):
-            wv[k] = weave("V" if k in v_self else "G", vp[k])
-        for k in (0, 1):
-            ws[k] = weave("S" if k in s_self else "G", sp[k])
-        for t in range(PACK):
-            cast(2, t)
-        for k in range(2, 7):
-            vp[k] = start(True, vorder[k][0], PAIRS[vorder[k][1]])
-            sp[k] = start(False, sorder[k][0], PAIRS[sorder[k][1]])
-            gather(True, vp[k], range(PACK))
-            gather(False, sp[k], range(PACK))
-            multiply(wv[k - 2])
-            multiply(ws[k - 2])
-            wv[k] = weave("V" if k in v_self else "G", vp[k])
-            ws[k] = weave("S" if k in s_self else "G", sp[k])
-        v7a = start(True, 1, (6,))
-        gather(True, v7a, range(PACK))
-        s7a = start(False, 2, (6,))
-        gather(False, s7a, range(PACK))
-        v7b = start(True, 1, (7,))
-        gather(True, v7b, range(PACK))
-        s7b = start(False, 2, (7,))
-        gather(False, s7b, range(PACK))
-        multiply(wv[5])
-        multiply(ws[5])
-        wva = weave("V", v7a)
-        multiply(wv[6])
-        wsa = weave("V", s7a)
-        multiply(ws[6])
-        multiply(wva)
-        wvb = weave("V", v7b)
-        multiply(wsa)
-        wsb = weave("V", s7b)
-        for e in range(6):
-            take_out(False, e)
-        multiply(wvb)
-        take_out(False, 6)
-        multiply(wsb)
-        take_out(True, 7)
+            nc.gpsimd.tensor_copy(xb3[:, t, :], st3[t // 2][:, t % 2, :])
+            for pc in va:
+                gather(True, pc, (t,))
+            for pc in sa:
+                gather(False, pc, (t,))
+        for a in range(2):
+            nc.gpsimd.tensor_copy(xb2[:, 2 * a : 2 * a + 2, :], st2[a][:])
+        nc.gpsimd.tensor_copy(xb1[:], raw[1][:, 2:4, :])
+        early = [weave("G", va[0], "slot_c"), weave("G", va[1], "slot_d"), weave("G", sa[0]), weave("G", sa[1])]
+
+        sc = [piece("slot_a", 2, LOW), piece("slot_b", 2, HIGH)]
+        vc0 = piece("vc_0", 1, LOW)
+        names = ("vc_a", "vc_b", "vc_c", "vc_d")
+        vct = [piece(names[i], 1, experts) for i, experts in enumerate(TAIL_PIECES)]
+        gather(True, vc0, (2, 3, 0, 1))
+        for pc in vct:
+            gather(True, pc, (2, 3), tuple(e for e in HIGH if e not in SHARED))
+        for pc in vct:
+            gather(True, pc, (0, 1))
+        for pc in sc:
+            gather(False, pc, range(PACK))
+        for pc in vct:
+            gather(False, pc, (2, 3), SHARED)
+
+        for pc in early:
+            multiply(pc)
+        w_vc0 = weave("V", vc0)
+        w_sc0 = weave("V", sc[0])
+        multiply(w_vc0)
+        multiply(w_sc0)
+        for e in LOW:
+            take_out(e)
+        w_sc1 = weave("V", sc[1])
+        w_t = [weave("V", vct[0])]
+        multiply(w_sc1)
+        for i in range(len(vct)):
+            if i + 1 < len(vct):
+                w_t.append(weave("V", vct[i + 1]))
+            multiply(w_t[i])
+            for e in vct[i][1]:
+                take_out(e)
 
         for h in range(T // HALF):
             cols = slice(h * HALF, (h + 1) * HALF)

@@ -25,7 +25,7 @@ LOW = (0, 1, 2, 3)
 HIGH = (4, 5, 6, 7)
 SHARED = (4, 5, 6, 7)
 TAIL_PIECES = ((4, 5), (6,), (7,))
-V_OUT = (4, 5, 6)
+V_OUT = (7,)
 
 
 def tile_routed_moe_kernel(tc, xT, w_words, w_scales, gate, offs, pos1, pos2, out):
@@ -56,7 +56,8 @@ def tile_routed_moe_kernel(tc, xT, w_words, w_scales, gate, offs, pos1, pos2, ou
         s_view = w_scales.rearrange("e a (q r) n -> a r q e n", r=4)
         gate_t = keep.tile([P, 2, T], F32, name="gate_t")
         acc = [psum.tile([P, C], F32, name="acc%d" % e) for e in range(E)]
-        y = keep.tile([P, SLOTS], F32, name="y")
+
+        y = keep.tile([P, SLOTS], F32, name="xb1")
 
         def piece(name, g, experts):
             u = keep.tile([P, PACK * C * len(experts)], BF16, name=name)

@@ -23,9 +23,13 @@ HALF = 512
 LIST_COLS = C // 16
 LOW = (0, 1, 2, 3)
 HIGH = (4, 5, 6, 7)
+WIDE = PACK * C * len(LOW)
 SHARED = (4, 5, 6, 7)
 TAIL_PIECES = ((4, 5), (6,), (7,))
 V_OUT = (7,)
+Q_WIDE = 4 * C
+Q_SLOT = PACK * Q_WIDE + Q_WIDE
+Q_SLOTS = 3
 
 
 def tile_routed_moe_kernel(tc, xT, w_words, w_scales, gate, offs, pos1, pos2, out):
@@ -33,8 +37,6 @@ def tile_routed_moe_kernel(tc, xT, w_words, w_scales, gate, offs, pos1, pos2, ou
     with ExitStack() as ctx:
         lists = ctx.enter_context(tc.tile_pool(name="lists", bufs=1))
         keep = ctx.enter_context(tc.tile_pool(name="keep", bufs=1))
-        woven = ctx.enter_context(tc.tile_pool(name="woven", bufs=3))
-        qring = ctx.enter_context(tc.tile_pool(name="qring", bufs=3))
         tail = ctx.enter_context(tc.tile_pool(name="tail", bufs=2))
         psum = ctx.enter_context(tc.psum_pool(name="psum", bufs=1))
 
@@ -44,12 +46,13 @@ def tile_routed_moe_kernel(tc, xT, w_words, w_scales, gate, offs, pos1, pos2, ou
         nc.sync.dma_start(offs_t[:], offs)
 
         x_view = xT.rearrange("(g p t) n -> g p t n", p=P, t=PACK)
-        raw = dict((g, keep.tile([P, PACK, T], F32, name="raw%d" % g)) for g in (0, 1))
+        raw0 = keep.tile([P, PACK, T], F32, name="raw0")
+        raw1 = keep.tile([P, PACK, T], F32, name="raw1", align_bytes=64)
         xb3 = keep.tile([P, PACK, T], BF16, name="xb3")
         xb2 = keep.tile([P, PACK, T], BF16, name="xb2")
         xb1 = keep.tile([P, 2, T], BF16, name="xb1")
         st3 = [keep.tile([P, 2, T], F32, name="slot_a"), keep.tile([P, 2, T], F32, name="slot_b")]
-        st2 = [keep.tile([P, 2, T], F32, name="slot_c", align_bytes=64), keep.tile([P, 2, T], F32, name="slot_d", align_bytes=64)]
+        st2 = keep.tile([P, PACK, T], F32, name="slot_c", align_bytes=64)
         w_codes = keep.tile([P, PASSES, E, N], I32, name="w_codes", align_bytes=64)
         w_planes = keep.tile([P, E * N], U8, name="w_planes", align_bytes=64)
         w_view = w_words.rearrange("e a p n r -> a p e (n r)")
@@ -57,15 +60,13 @@ def tile_routed_moe_kernel(tc, xT, w_words, w_scales, gate, offs, pos1, pos2, ou
         gate_t = keep.tile([P, 2, T], F32, name="gate_t")
         acc = [psum.tile([P, C], F32, name="acc%d" % e) for e in range(E)]
 
-        y = keep.tile([P, SLOTS], F32, name="xb1")
-
         def piece(name, g, experts):
             u = keep.tile([P, PACK * C * len(experts)], BF16, name=name)
-            return (g, experts, u)
+            return (g, experts, u[:])
 
-        def gather(on_vector, pc, planes, only=None):
+        def gather(on_vector, pc, planes, only=None, late=False):
             g, experts, u = pc
-            view = u[:].rearrange("p (h n e) -> p h n e", h=2, e=2)
+            view = u.rearrange("p (h n e) -> p h n e", h=2, e=2)
             for t in planes:
                 for j, e in enumerate(experts):
                     if only is not None and e not in only:
@@ -73,19 +74,17 @@ def tile_routed_moe_kernel(tc, xT, w_words, w_scales, gate, offs, pos1, pos2, ou
                     dst = view[:, t // 2, j * C : (j + 1) * C, t % 2]
                     lst = offs_t[:, e * LIST_COLS : (e + 1) * LIST_COLS]
                     if on_vector:
-                        nc.vector.tensor_copy(dst, raw[g][:, t, :].indirect(lst))
+                        window = raw0[:, t, :] if g == 0 else raw1[:, t, :]
+                        nc.vector.tensor_copy(dst, window.indirect(lst))
                     else:
                         window = xb3[:, t, :] if g == 3 else (xb2[:, t, :] if g == 2 else xb1[:, t - 2, :])
                         nc.scalar.activation(dst, window.indirect(lst), COPY)
 
-        def weave(engine, pc, slot=None):
+        def weave(engine, pc, place):
             g, experts, u = pc
-            if slot is None:
-                gr = woven.tile([P, PACK * C * len(experts)], BF16, name="gr", align_bytes=64)
-            else:
-                gr = keep.tile([P, PACK * C * len(experts)], BF16, name=slot, align_bytes=64)
-            dst = gr[:].bitcast(F32).rearrange("p (n h) -> p n h", h=2)
-            src = u[:].bitcast(F32).rearrange("p (h n) -> p n h", h=2)
+            gr = place
+            dst = gr.bitcast(F32).rearrange("p (n h) -> p n h", h=2)
+            src = u.bitcast(F32).rearrange("p (h n) -> p n h", h=2)
             if engine == "S":
                 nc.scalar.copy(dst, src)
             elif engine == "V":
@@ -94,37 +93,36 @@ def tile_routed_moe_kernel(tc, xT, w_words, w_scales, gate, offs, pos1, pos2, ou
                 nc.gpsimd.tensor_copy(dst, src)
             return (g, experts, gr)
 
+        used = [0]
+        q_all = []
+
         def multiply(pc):
             g, experts, gr = pc
             n = C * len(experts)
-            codes = qring.tile([P, n], I32, name="codes", align_bytes=64)
-            scales = qring.tile([P, n], U8, name="scales", align_bytes=64)
-            nc.vector.quantize_mx(out=codes[:].bitcast(FP8X4), scales=scales[:], in_=gr[:])
+            base = Q_SLOT * (used[0] % Q_SLOTS)
+            used[0] += 1
+            codes = q_all[0][:, base : base + PACK * n]
+            scales = q_all[0][:, base + PACK * Q_WIDE : base + PACK * Q_WIDE + n]
+            nc.vector.quantize_mx(out=codes.bitcast(FP8X4), scales=scales, in_=gr)
             for j, e in enumerate(experts):
                 nc.tensor.matmul_mx(
                     out=acc[e][:],
                     lhsT=w_codes[:, g, e, :].bitcast(FP8X4),
                     lhsT_scale=w_planes[4 * g : P, e * N : (e + 1) * N],
-                    rhs=codes[:, j * C : (j + 1) * C].bitcast(FP8X4),
+                    rhs=codes[:, PACK * j * C : PACK * (j + 1) * C].bitcast(FP8X4),
                     rhs_scale=scales[:, j * C : (j + 1) * C],
                     start=(g == 0),
                     stop=(g == (2 if e in LOW else 1)),
                 )
 
-        def take_out(e):
-            if e in V_OUT:
-                nc.vector.tensor_copy(y[:, e * C : (e + 1) * C], acc[e][:])
-            else:
-                nc.scalar.copy(y[:, e * C : (e + 1) * C], acc[e][:])
-
         nc.vector.memset(w_planes[:].bitcast(I32), 0)
         for t in range(PACK):
-            nc.sync.dma_start(raw[0][:, t, :], x_view[0, :, t, :])
+            nc.sync.dma_start(raw0[:, t, :], x_view[0, :, t, :])
             nc.sync.dma_start(st3[t // 2][:, t % 2, :], x_view[3, :, t, :])
         for t in range(PACK):
-            nc.sync.dma_start(st2[t // 2][:, t % 2, :], x_view[2, :, t, :])
+            nc.sync.dma_start(st2[:, t, :], x_view[2, :, t, :])
         for t in (2, 3, 0, 1):
-            nc.sync.dma_start(raw[1][:, t, :], x_view[1, :, t, :])
+            nc.sync.dma_start(raw1[:, t, :], x_view[1, :, t, :])
         for a in range(PASSES):
             for r in range(4):
                 nc.sync.dma_start(
@@ -146,9 +144,10 @@ def tile_routed_moe_kernel(tc, xT, w_words, w_scales, gate, offs, pos1, pos2, ou
             for pc in sa:
                 gather(False, pc, (t,))
         for a in range(2):
-            nc.gpsimd.tensor_copy(xb2[:, 2 * a : 2 * a + 2, :], st2[a][:])
-        nc.gpsimd.tensor_copy(xb1[:], raw[1][:, 2:4, :])
-        early = [weave("G", va[0], "slot_c"), weave("G", va[1], "slot_d"), weave("G", sa[0]), weave("G", sa[1])]
+            nc.gpsimd.tensor_copy(xb2[:, 2 * a : 2 * a + 2, :], st2[:, 2 * a : 2 * a + 2, :])
+        early_all = keep.tile([P, 4 * WIDE], BF16, name="slot_c", align_bytes=64)
+        early = [weave("G", pc, early_all[:, i * WIDE : (i + 1) * WIDE]) for i, pc in enumerate((va[0], va[1], sa[0], sa[1]))]
+        nc.gpsimd.tensor_copy(xb1[:], raw1[:, 2:4, :])
 
         sc = [piece("slot_a", 2, LOW), piece("slot_b", 2, HIGH)]
         vc0 = piece("vc_0", 1, LOW)
@@ -158,26 +157,41 @@ def tile_routed_moe_kernel(tc, xT, w_words, w_scales, gate, offs, pos1, pos2, ou
         for pc in vct:
             gather(True, pc, (2, 3), tuple(e for e in HIGH if e not in SHARED))
         for pc in vct:
-            gather(True, pc, (0, 1))
+            gather(True, pc, (0, 1), None, True)
         for pc in sc:
             gather(False, pc, range(PACK))
         for pc in vct:
             gather(False, pc, (2, 3), SHARED)
 
+        y = keep.tile([P, SLOTS], F32, name="xb1")
+
+        def take_out(e):
+            if e in V_OUT:
+                nc.vector.tensor_copy(y[:, e * C : (e + 1) * C], acc[e][:])
+            else:
+                nc.scalar.copy(y[:, e * C : (e + 1) * C], acc[e][:])
+
+        q_all.append(keep.tile([P, Q_SLOTS * Q_SLOT], U8, name="raw1", align_bytes=64))
         for pc in early:
             multiply(pc)
-        w_vc0 = weave("V", vc0)
-        w_sc0 = weave("V", sc[0])
+        late_all = keep.tile([P, 4 * WIDE], BF16, name="slot_c", align_bytes=64)
+        places = []
+        at = 3 * WIDE
+        for experts in TAIL_PIECES:
+            places.append(late_all[:, at : at + PACK * C * len(experts)])
+            at += PACK * C * len(experts)
+        w_vc0 = weave("V", vc0, late_all[:, 0:WIDE])
+        w_sc0 = weave("V", sc[0], late_all[:, WIDE : 2 * WIDE])
         multiply(w_vc0)
         multiply(w_sc0)
         for e in LOW:
             take_out(e)
-        w_sc1 = weave("V", sc[1])
-        w_t = [weave("V", vct[0])]
+        w_sc1 = weave("V", sc[1], late_all[:, 2 * WIDE : 3 * WIDE])
+        w_t = [weave("V", vct[0], places[0])]
         multiply(w_sc1)
         for i in range(len(vct)):
             if i + 1 < len(vct):
-                w_t.append(weave("V", vct[i + 1]))
+                w_t.append(weave("V", vct[i + 1], places[i + 1]))
             multiply(w_t[i])
             for e in vct[i][1]:
                 take_out(e)

@@ -118,11 +118,16 @@ def tile_routed_moe_kernel(tc, xT, w_words, w_scales, gate, offs, pos1, pos2, ou
         nc.vector.memset(w_planes[:].bitcast(I32), 0)
         for t in range(PACK):
             nc.sync.dma_start(raw0[:, t, :], x_view[0, :, t, :])
-            nc.sync.dma_start(st3[t // 2][:, t % 2, :], x_view[3, :, t, :])
+            if t == 0:
+                nc.sync.dma_start(st3[0][:, 0, 0:HALF], x_view[3, :, 0, 0:HALF])
+                nc.sync.dma_start(st3[0][:, 0, HALF:T], x_view[3, :, 0, HALF:T])
+            else:
+                nc.sync.dma_start(st3[t // 2][:, t % 2, :], x_view[3, :, t, :])
         for t in range(PACK):
             nc.sync.dma_start(st2[:, t, :], x_view[2, :, t, :])
-        for t in (2, 3, 0, 1):
+        for t in (2, 3):
             nc.sync.dma_start(raw1[:, t, :], x_view[1, :, t, :])
+        nc.sync.dma_start(raw1[:, 0:2, :], x_view[1, :, 0:2, :])
         for a in range(PASSES):
             for r in range(4):
                 nc.sync.dma_start(
@@ -138,7 +143,11 @@ def tile_routed_moe_kernel(tc, xT, w_words, w_scales, gate, offs, pos1, pos2, ou
         va = [piece("va0", 0, LOW), piece("va1", 0, HIGH)]
         sa = [piece("sa0", 3, LOW), piece("sa1", 3, HIGH)]
         for t in range(PACK):
-            nc.gpsimd.tensor_copy(xb3[:, t, :], st3[t // 2][:, t % 2, :])
+            if t == 0:
+                nc.gpsimd.tensor_copy(xb3[:, 0, 0:HALF], st3[0][:, 0, 0:HALF])
+                nc.scalar.copy(xb3[:, 0, HALF:T], st3[0][:, 0, HALF:T])
+            else:
+                nc.gpsimd.tensor_copy(xb3[:, t, :], st3[t // 2][:, t % 2, :])
             for pc in va:
                 gather(True, pc, (t,))
             for pc in sa:
@@ -154,6 +163,8 @@ def tile_routed_moe_kernel(tc, xT, w_words, w_scales, gate, offs, pos1, pos2, ou
         names = ("vc_a", "vc_b", "vc_c", "vc_d")
         vct = [piece(names[i], 1, experts) for i, experts in enumerate(TAIL_PIECES)]
         gather(True, vc0, (2, 3, 0, 1))
+        vc0_woven = keep.tile([P, WIDE], BF16, name="vc0_woven", align_bytes=64)
+        w_vc0 = weave("G", vc0, vc0_woven[:])
         for pc in vct:
             gather(True, pc, (2, 3), tuple(e for e in HIGH if e not in SHARED))
         for pc in vct:
@@ -180,7 +191,6 @@ def tile_routed_moe_kernel(tc, xT, w_words, w_scales, gate, offs, pos1, pos2, ou
         for experts in TAIL_PIECES:
             places.append(late_all[:, at : at + PACK * C * len(experts)])
             at += PACK * C * len(experts)
-        w_vc0 = weave("V", vc0, late_all[:, 0:WIDE])
         w_sc0 = weave("V", sc[0], late_all[:, WIDE : 2 * WIDE])
         multiply(w_vc0)
         multiply(w_sc0)

@@ -24,7 +24,6 @@ LIST_COLS = C // 16
 LOW = (0, 1, 2, 3)
 HIGH = (4, 5, 6, 7)
 WIDE = PACK * C * len(LOW)
-SHARED = (4, 5, 6, 7)
 TAIL_PIECES = ((4, 5), (6,), (7,))
 V_OUT = (7,)
 Q_WIDE = 4 * C
@@ -64,15 +63,15 @@ def tile_routed_moe_kernel(tc, xT, w_words, w_scales, gate, offs, pos1, pos2, ou
             u = keep.tile([P, PACK * C * len(experts)], BF16, name=name)
             return (g, experts, u[:])
 
-        def gather(on_vector, pc, planes, only=None, late=False):
+        def gather(on_vector, pc, planes, only=None, lo=0, hi=C):
             g, experts, u = pc
             view = u.rearrange("p (h n e) -> p h n e", h=2, e=2)
             for t in planes:
                 for j, e in enumerate(experts):
                     if only is not None and e not in only:
                         continue
-                    dst = view[:, t // 2, j * C : (j + 1) * C, t % 2]
-                    lst = offs_t[:, e * LIST_COLS : (e + 1) * LIST_COLS]
+                    dst = view[:, t // 2, j * C + lo : j * C + hi, t % 2]
+                    lst = offs_t[:, e * LIST_COLS + lo // 16 : e * LIST_COLS + hi // 16]
                     if on_vector:
                         window = raw0[:, t, :] if g == 0 else raw1[:, t, :]
                         nc.vector.tensor_copy(dst, window.indirect(lst))
@@ -152,27 +151,32 @@ def tile_routed_moe_kernel(tc, xT, w_words, w_scales, gate, offs, pos1, pos2, ou
                 gather(True, pc, (t,))
             for pc in sa:
                 gather(False, pc, (t,))
-        for a in range(2):
-            nc.gpsimd.tensor_copy(xb2[:, 2 * a : 2 * a + 2, :], st2[:, 2 * a : 2 * a + 2, :])
+        nc.gpsimd.tensor_copy(xb2[:], st2[:])
         early_all = keep.tile([P, 4 * WIDE], BF16, name="slot_c", align_bytes=64)
         early = [weave("G", pc, early_all[:, i * WIDE : (i + 1) * WIDE]) for i, pc in enumerate((va[0], va[1], sa[0], sa[1]))]
         nc.gpsimd.tensor_copy(xb1[:], raw1[:, 2:4, :])
 
-        sc = [piece("slot_a", 2, LOW), piece("slot_b", 2, HIGH)]
+        sc_low = keep.tile([P, WIDE], BF16, name="slot_a")
+        sc_a = (2, (0, 1), sc_low[:, 0 : WIDE // 2])
+        sc_b = (2, (2, 3), sc_low[:, WIDE // 2 :])
+        sc_high = piece("slot_b", 2, HIGH)
         vc0 = piece("vc_0", 1, LOW)
         names = ("vc_a", "vc_b", "vc_c", "vc_d")
         vct = [piece(names[i], 1, experts) for i, experts in enumerate(TAIL_PIECES)]
         gather(True, vc0, (2, 3, 0, 1))
         vc0_woven = keep.tile([P, WIDE], BF16, name="vc0_woven", align_bytes=64)
         w_vc0 = weave("G", vc0, vc0_woven[:])
+        gather(True, vct[0], (2, 3), (4,), 0, C // 2)
         for pc in vct:
-            gather(True, pc, (2, 3), tuple(e for e in HIGH if e not in SHARED))
+            gather(True, pc, (0, 1))
+        gather(False, sc_a, range(PACK))
+        sc_a_woven = keep.tile([P, WIDE // 2], BF16, name="sc_a_woven", align_bytes=64)
+        w_sc_a = weave("G", sc_a, sc_a_woven[:])
+        gather(False, sc_b, range(PACK))
+        gather(False, sc_high, range(PACK))
+        gather(False, vct[0], (2, 3), (4,), C // 2, C)
         for pc in vct:
-            gather(True, pc, (0, 1), None, True)
-        for pc in sc:
-            gather(False, pc, range(PACK))
-        for pc in vct:
-            gather(False, pc, (2, 3), SHARED)
+            gather(False, pc, (2, 3), (5, 6, 7))
 
         y = keep.tile([P, SLOTS], F32, name="xb1")
 
@@ -191,12 +195,13 @@ def tile_routed_moe_kernel(tc, xT, w_words, w_scales, gate, offs, pos1, pos2, ou
         for experts in TAIL_PIECES:
             places.append(late_all[:, at : at + PACK * C * len(experts)])
             at += PACK * C * len(experts)
-        w_sc0 = weave("V", sc[0], late_all[:, WIDE : 2 * WIDE])
+        w_sc_b = weave("V", sc_b, late_all[:, WIDE : WIDE + WIDE // 2])
         multiply(w_vc0)
-        multiply(w_sc0)
+        multiply(w_sc_a)
+        multiply(w_sc_b)
         for e in LOW:
             take_out(e)
-        w_sc1 = weave("V", sc[1], late_all[:, 2 * WIDE : 3 * WIDE])
+        w_sc1 = weave("V", sc_high, late_all[:, 2 * WIDE : 3 * WIDE])
         w_t = [weave("V", vct[0], places[0])]
         multiply(w_sc1)
         for i in range(len(vct)):

from contextlib import ExitStack

import concourse.mybir as mybir

K, T, E, C, N = 2048, 1024, 8, 256, 128
FLOPS = 2 * K * E * C * N

F32 = mybir.dt.float32
BF16 = mybir.dt.bfloat16
I32 = mybir.dt.int32
U8 = mybir.dt.uint8
U16 = mybir.dt.uint16
FP8X4 = mybir.dt.float8_e4m3fn_x4
MULT = mybir.AluOpType.mult
ADD = mybir.AluOpType.add
COPY = mybir.ActivationFunctionType.Copy

P = 128
PACK = 4
PASSES = K // (P * PACK)
SLOTS = E * C
HALF = 512
LIST_COLS = C // 16
LOW = (0, 1, 2, 3)
HIGH = (4, 5, 6, 7)
WIDE = PACK * C * len(LOW)
TAIL_PIECES = ((4, 5), (6,), (7,))
V_OUT = (7,)
Q_WIDE = 4 * C
Q_SLOT = PACK * Q_WIDE + Q_WIDE
Q_SLOTS = 3


def tile_routed_moe_kernel(tc, xT, w_words, w_scales, gate, offs, pos1, pos2, out):
    nc = tc.nc
    with ExitStack() as ctx:
        lists = ctx.enter_context(tc.tile_pool(name="lists", bufs=1))
        keep = ctx.enter_context(tc.tile_pool(name="keep", bufs=1))
        tail = ctx.enter_context(tc.tile_pool(name="tail", bufs=2))
        psum = ctx.enter_context(tc.psum_pool(name="psum", bufs=1))

        offs_t = lists.tile([P, SLOTS // 16], U16, name="offs_t")
        pos1_t = lists.tile([P, T // 16], U16, name="pos1_t")
        pos2_t = lists.tile([P, T // 16], U16, name="pos2_t")
        nc.sync.dma_start(offs_t[:], offs)

        x_view = xT.rearrange("(g p t) n -> g p t n", p=P, t=PACK)
        raw0 = keep.tile([P, PACK, T], F32, name="raw0")
        raw1 = keep.tile([P, PACK, T], F32, name="raw1", align_bytes=64)
        xb3 = keep.tile([P, PACK, T], BF16, name="xb3")
        xb2 = keep.tile([P, PACK, T], BF16, name="xb2")
        xb1 = keep.tile([P, 2, T], BF16, name="xb1")
        st3 = [keep.tile([P, 2, T], F32, name="slot_a"), keep.tile([P, 2, T], F32, name="slot_b")]
        st2 = keep.tile([P, PACK, T], F32, name="slot_c", align_bytes=64)
        w_codes = keep.tile([P, PASSES, E, N], I32, name="w_codes", align_bytes=64)
        w_planes = keep.tile([P, E * N], U8, name="w_planes", align_bytes=64)
        w_view = w_words.rearrange("e a p n r -> a p e (n r)")
        s_view = w_scales.rearrange("e a (q r) n -> a r q e n", r=4)
        gate_t = keep.tile([P, 2, T], F32, name="gate_t")
        acc = [psum.tile([P, C], F32, name="acc%d" % e) for e in range(E)]

        def piece(name, g, experts):
            u = keep.tile([P, PACK * C * len(experts)], BF16, name=name)
            return (g, experts, u[:])

        def gather(on_vector, pc, planes, only=None, lo=0, hi=C):
            g, experts, u = pc
            view = u.rearrange("p (h n e) -> p h n e", h=2, e=2)
            for t in planes:
                for j, e in enumerate(experts):
                    if only is not None and e not in only:
                        continue
                    dst = view[:, t // 2, j * C + lo : j * C + hi, t % 2]
                    lst = offs_t[:, e * LIST_COLS + lo // 16 : e * LIST_COLS + hi // 16]
                    if on_vector:
                        window = raw0[:, t, :] if g == 0 else raw1[:, t, :]
                        nc.vector.tensor_copy(dst, window.indirect(lst))
                    else:
                        window = xb3[:, t, :] if g == 3 else (xb2[:, t, :] if g == 2 else xb1[:, t - 2, :])
                        nc.scalar.activation(dst, window.indirect(lst), COPY)

        def weave(engine, pc, place):
            g, experts, u = pc
            gr = place
            dst = gr.bitcast(F32).rearrange("p (n h) -> p n h", h=2)
            src = u.bitcast(F32).rearrange("p (h n) -> p n h", h=2)
            if engine == "S":
                nc.scalar.copy(dst, src)
            elif engine == "V":
                nc.vector.tensor_copy(dst, src)
            else:
                nc.gpsimd.tensor_copy(dst, src)
            return (g, experts, gr)

        used = [0]
        q_all = []

        def multiply(pc):
            g, experts, gr = pc
            n = C * len(experts)
            base = Q_SLOT * (used[0] % Q_SLOTS)
            used[0] += 1
            codes = q_all[0][:, base : base + PACK * n]
            scales = q_all[0][:, base + PACK * Q_WIDE : base + PACK * Q_WIDE + n]
            nc.vector.quantize_mx(out=codes.bitcast(FP8X4), scales=scales, in_=gr)
            for j, e in enumerate(experts):
                nc.tensor.matmul_mx(
                    out=acc[e][:],
                    lhsT=w_codes[:, g, e, :].bitcast(FP8X4),
                    lhsT_scale=w_planes[4 * g : P, e * N : (e + 1) * N],
                    rhs=codes[:, PACK * j * C : PACK * (j + 1) * C].bitcast(FP8X4),
                    rhs_scale=scales[:, j * C : (j + 1) * C],
                    start=(g == 0),
                    stop=(g == (2 if e in LOW else 1)),
                )

        nc.vector.memset(w_planes[:].bitcast(I32), 0)
        for t in range(PACK):
            nc.sync.dma_start(raw0[:, t, :], x_view[0, :, t, :])
            if t == 0:
                nc.sync.dma_start(st3[0][:, 0, 0:HALF], x_view[3, :, 0, 0:HALF])
                nc.sync.dma_start(st3[0][:, 0, HALF:T], x_view[3, :, 0, HALF:T])
            else:
                nc.sync.dma_start(st3[t // 2][:, t % 2, :], x_view[3, :, t, :])
        for t in range(PACK):
            nc.sync.dma_start(st2[:, t, :], x_view[2, :, t, :])
        for t in (2, 3):
            nc.sync.dma_start(raw1[:, t, :], x_view[1, :, t, :])
        nc.sync.dma_start(raw1[:, 0:2, :], x_view[1, :, 0:2, :])
        for a in range(PASSES):
            for r in range(4):
                nc.sync.dma_start(
                    w_planes[4 * a + r : P : 32, :].rearrange("q (e n) -> q e n", e=E).bitcast(I32),
                    s_view[a, r].bitcast(I32),
                )
        for g in (0, 3, 1, 2):
            nc.sync.dma_start(w_codes[:, g, :, :], w_view[g].bitcast(I32))
        nc.sync.dma_start(pos1_t[:], pos1)
        nc.sync.dma_start(pos2_t[:], pos2)
        nc.sync.dma_start(gate_t[:], gate.rearrange("r n t -> n r t"))

        va = [piece("va0", 0, LOW), piece("va1", 0, HIGH)]
        sa = [piece("sa0", 3, LOW), piece("sa1", 3, HIGH)]
        for t in range(PACK):
            if t == 0:
                nc.gpsimd.tensor_copy(xb3[:, 0, 0:HALF], st3[0][:, 0, 0:HALF])
                nc.scalar.copy(xb3[:, 0, HALF:T], st3[0][:, 0, HALF:T])
            else:
                nc.gpsimd.tensor_copy(xb3[:, t, :], st3[t // 2][:, t % 2, :])
            for pc in va:
                gather(True, pc, (t,))
            for pc in sa:
                gather(False, pc, (t,))
        nc.gpsimd.tensor_copy(xb2[:], st2[:])
        early_all = keep.tile([P, 4 * WIDE], BF16, name="slot_c", align_bytes=64)
        early = [weave("G", pc, early_all[:, i * WIDE : (i + 1) * WIDE]) for i, pc in enumerate((va[0], va[1], sa[0], sa[1]))]
        nc.gpsimd.tensor_copy(xb1[:], raw1[:, 2:4, :])

        sc_low = keep.tile([P, WIDE], BF16, name="slot_a")
        sc_a = (2, (0, 1), sc_low[:, 0 : WIDE // 2])
        sc_b = (2, (2, 3), sc_low[:, WIDE // 2 :])
        sc_high = piece("slot_b", 2, HIGH)
        vc0 = piece("vc_0", 1, LOW)
        names = ("vc_a", "vc_b", "vc_c", "vc_d")
        vct = [piece(names[i], 1, experts) for i, experts in enumerate(TAIL_PIECES)]
        gather(True, vc0, (2, 3, 0, 1))
        vc0_woven = keep.tile([P, WIDE], BF16, name="vc0_woven", align_bytes=64)
        w_vc0 = weave("G", vc0, vc0_woven[:])
        gather(True, vct[0], (2, 3), (4,), 0, C // 2)
        for pc in vct:
            gather(True, pc, (0, 1))
        gather(False, sc_a, range(PACK))
        sc_a_woven = keep.tile([P, WIDE // 2], BF16, name="sc_a_woven", align_bytes=64)
        w_sc_a = weave("G", sc_a, sc_a_woven[:])
        gather(False, sc_b, range(PACK))
        gather(False, sc_high, range(PACK))
        gather(False, vct[0], (2, 3), (4,), C // 2, C)
        for pc in vct:
            gather(False, pc, (2, 3), (5, 6, 7))

        y = keep.tile([P, SLOTS], F32, name="xb1")

        def take_out(e):
            if e in V_OUT:
                nc.vector.tensor_copy(y[:, e * C : (e + 1) * C], acc[e][:])
            else:
                nc.scalar.copy(y[:, e * C : (e + 1) * C], acc[e][:])

        q_all.append(keep.tile([P, Q_SLOTS * Q_SLOT], U8, name="raw1", align_bytes=64))
        for pc in early:
            multiply(pc)
        late_all = keep.tile([P, 4 * WIDE], BF16, name="slot_c", align_bytes=64)
        places = []
        at = 3 * WIDE
        for experts in TAIL_PIECES:
            places.append(late_all[:, at : at + PACK * C * len(experts)])
            at += PACK * C * len(experts)
        w_sc_b = weave("V", sc_b, late_all[:, WIDE : WIDE + WIDE // 2])
        multiply(w_vc0)
        multiply(w_sc_a)
        multiply(w_sc_b)
        for e in LOW:
            take_out(e)
        w_sc1 = weave("V", sc_high, late_all[:, 2 * WIDE : 3 * WIDE])
        w_t = [weave("V", vct[0], places[0])]
        multiply(w_sc1)
        for i in range(len(vct)):
            if i + 1 < len(vct):
                w_t.append(weave("V", vct[i + 1], places[i + 1]))
            multiply(w_t[i])
            for e in vct[i][1]:
                take_out(e)

        for h in range(T // HALF):
            cols = slice(h * HALF, (h + 1) * HALF)
            lcols = slice(h * (HALF // 16), (h + 1) * (HALF // 16))
            z1 = tail.tile([P, HALF], F32, name="z1")
            z2 = tail.tile([P, HALF], F32, name="z2")
            nc.vector.tensor_tensor(z1[:], y[:].indirect(pos1_t[:, lcols]), gate_t[:, 0, cols], MULT)
            nc.vector.tensor_tensor(z2[:], y[:].indirect(pos2_t[:, lcols]), gate_t[:, 1, cols], MULT)
            res = tail.tile([P, HALF], F32, name="res")
            nc.vector.tensor_tensor(res[:], z1[:], z2[:], ADD)
            nc.sync.dma_start(out[:, cols], res[:])
